import numpy as np
import ml_dtypes


def mxq(x, axis, fmt="e4m3"):
    dtype, down = {"e4m3": (ml_dtypes.float8_e4m3fn, 7), "e5m2": (ml_dtypes.float8_e5m2, 14)}[fmt]
    v = np.moveaxis(np.asarray(x, np.float32).astype(ml_dtypes.bfloat16).astype(np.float64), axis, -1)
    blocks = v.reshape(v.shape[:-1] + (-1, 32))
    amax = np.abs(blocks).max(-1, keepdims=True)
    byte = np.maximum(np.where(amax > 0, np.frexp(amax)[1] - 1 + 127, 0) - down, 1)
    scale = np.exp2(byte - 127.0)
    codes = (blocks / scale).astype(np.float32).astype(dtype).astype(np.float64)
    return np.moveaxis((codes * scale).reshape(v.shape), -1, axis)


WIDE = False


def mx_kscale(k):
    if not WIDE:
        return np.ones(k)
    levels = np.array([10, -10, 5, -5, 0])
    if k % 512:
        return np.exp2(np.random.permutation(np.resize(levels, k // 32))).repeat(32)
    a = np.empty((k // 512, 16))
    for p in range(k // 512):
        a[p, :8] = np.random.permutation(np.resize(levels, 8))
        for g in range(8):
            far = levels[np.abs(levels - a[p, g]) >= 10]
            a[p, g + 8] = far[np.random.randint(len(far))]
    return np.exp2(a.ravel()).repeat(32)


def f64(x):
    return np.asarray(x).astype(np.float64)


def striped(idx):
    return np.tile(idx.reshape(-1, 16).T, (8, 1)).astype(np.uint16)


def unstriped(offs):
    return offs[:16].T.reshape(-1).astype(np.int64)


E2M1 = np.array([0.0, 0.5, 1.0, 1.5, 2.0, 3.0, 4.0, 6.0, -0.0, -0.5, -1.0, -1.5, -2.0, -3.0, -4.0, -6.0])


def pack_weight(w, fmt):
    k, n = w.shape
    w = f64(np.asarray(w, np.float32).astype(ml_dtypes.bfloat16)).reshape(k // 32, 32, n)
    amax = np.abs(w).max(1)
    if fmt == "e4m3":
        byte = np.frexp(amax)[1] - 1 + 127 - 7
    else:
        mant, ex = np.frexp(amax / 6.0)
        byte = np.where(mant > 0.5, ex, ex - 1) + 127
    byte = np.clip(np.where(amax > 0, byte, 1), 1, 254)
    scaled = (w * np.exp2(127.0 - byte)[:, None, :]).reshape(k, n).astype(np.float32)
    by_word = np.ascontiguousarray(scaled.reshape(k // 512, 128, 4, n).transpose(0, 1, 3, 2))
    if fmt == "e4m3":
        words = by_word.astype(ml_dtypes.float8_e4m3fn).view(np.uint8)
    else:
        c = by_word.astype(ml_dtypes.float4_e2m1fn).view(np.uint8) & 0xF
        words = (c[..., 0::2] | (c[..., 1::2] << 4)).reshape(k // 512, 128, 2 * n)
    return np.ascontiguousarray(words), np.ascontiguousarray(byte.astype(np.uint8).reshape(k // 512, 16, n))


def unpack_weight(words, scales, fmt):
    g, _, n = scales.shape
    words = np.ascontiguousarray(words).reshape(g, 128, n, -1)
    if fmt == "e4m3":
        vals = words.view(ml_dtypes.float8_e4m3fn).astype(np.float64)
    else:
        nib = np.empty((g, 128, n, 4), np.uint8)
        nib[..., 0::2] = words & 0xF
        nib[..., 1::2] = words >> 4
        vals = E2M1[nib]
    vals = vals * np.repeat(np.exp2(scales.astype(np.float64) - 127.0), 8, axis=1)[..., None]
    return vals.transpose(0, 1, 3, 2).reshape(g * 512, n)


def gelu(v):
    return 0.5 * v * (1.0 + np.tanh(np.sqrt(2.0 / np.pi) * (v + 0.044715 * v**3)))


def bf(x):
    return np.asarray(x, np.float32).astype(ml_dtypes.bfloat16)


def planes(Y):
    n, m = Y.shape
    b = f64(bf(Y)).reshape(n // 32, 32, m)
    amax = np.abs(b).max(1)
    byte = np.clip(np.where(amax > 0, np.frexp(amax)[1] - 1 + 127 - 7, 1), 1, 254)
    codes = (b * np.exp2(127.0 - byte)[:, None, :]).reshape(n, m).astype(np.float32).astype(ml_dtypes.float8_e4m3fn).view(np.uint8)
    words = codes.reshape(n // 512, 128, 4, m).transpose(0, 1, 3, 2)
    return np.ascontiguousarray(words), np.ascontiguousarray(byte.astype(np.uint8).reshape(n // 512, 16, m))


K, H, N, T, S, P = 1024, 1024, 512, 4096, 1024, 512


def setup_inputs():
    n = np.random.standard_normal
    s = mx_kscale(K)[:, None]
    u = mx_kscale(H)[:, None]
    tab_words, tab_scales = pack_weight(n((K, T)) * s, "e4m3")
    w1 = (1.3 * n((K, H)) / np.sqrt(K) / s).astype(np.float32)
    hgain = (np.random.uniform(0.5, 2.0, H) * u[:, 0]).astype(np.float32)
    wa_words, wa_scales = pack_weight(0.8 * n((H, N)) / np.sqrt(H) / u, "e2m1")
    wb_words, wb_scales = pack_weight(1.5 * n((K, N)) / np.sqrt(K) / s, "e4m3")
    return {
        "tab_words": tab_words, "tab_scales": tab_scales,
        "offs": striped(np.random.permutation(T)[:S]),
        "w1": w1, "hgain": hgain,
        "wa_words": wa_words, "wa_scales": wa_scales,
        "wb_words": wb_words, "wb_scales": wb_scales,
        "pos1": striped(np.random.permutation(S)[:P]),
        "pos2": striped(np.random.permutation(S)[:P]),
        "temp": np.random.uniform(0.4, 1.6, N).astype(np.float32),
        "shift": (0.5 * n(N)).astype(np.float32),
        "mat": np.random.uniform(0.5, 2.0, (N, P)).astype(np.float32),
        "ygain": (0.5 * np.exp(0.8 * n(N))).astype(np.float32),
    }


def reference(tab_words, tab_scales, offs, w1, hgain, wa_words, wa_scales, wb_words, wb_scales,
              pos1, pos2, temp, shift, mat, ygain):
    v = unpack_weight(tab_words, tab_scales, "e4m3")[:, unstriped(offs)]
    wa = unpack_weight(wa_words, wa_scales, "e2m1")
    wb = unpack_weight(wb_words, wb_scales, "e4m3")
    h = np.tanh(mxq(f64(w1), 0, "e4m3").T @ v) * f64(hgain)[:, None]
    hq = mxq(h, 0, "e4m3")
    e = wa.T @ hq
    d = wb.T @ v
    a = np.exp(f64(temp)[:, None] * e[:, unstriped(pos1)] + f64(shift)[:, None])
    c = d[:, unstriped(pos2)] * f64(mat)
    y = f64(ygain)[:, None] * (c - a)
    words, scales = planes(y)
    return y, words, scales

@@ -1,0 +1,296 @@
+from contextlib import ExitStack
+
+import concourse.mybir as mybir
+
+K, H, N, T, S, M = 1024, 1024, 512, 4096, 1024, 512
+FLOPS = 2 * K * H * S + 2 * H * N * S + 2 * K * N * S
+
+F32 = mybir.dt.float32
+BF16 = mybir.dt.bfloat16
+I32 = mybir.dt.int32
+U32 = mybir.dt.uint32
+U16 = mybir.dt.uint16
+U8 = mybir.dt.uint8
+FP8X4 = mybir.dt.float8_e4m3fn_x4
+FP4X4 = mybir.dt.float4_e2m1fn_x4
+ACT = mybir.ActivationFunctionType
+ALU = mybir.AluOpType
+
+P = 128
+PACK = 4
+PASS = P * PACK
+BANK = 512
+UNIT = 256
+HALF = 256
+
+
+def tile_list_tariff_spike_scores_kernel(
+    tc, tab_words, tab_scales, offs, w1, hgain, wa_words, wa_scales, wb_words, wb_scales,
+    pos1, pos2, temp, shift, mat, ygain, out_0, out_1, out_2,
+):
+    nc = tc.nc
+    with ExitStack() as ctx:
+        lists = ctx.enter_context(tc.tile_pool(name="lists", bufs=1))
+        keep = ctx.enter_context(tc.tile_pool(name="keep", bufs=1))
+        stage = ctx.enter_context(tc.tile_pool(name="stage", bufs=1))
+        ring = ctx.enter_context(tc.tile_pool(name="ring", bufs=1))
+        psum = ctx.enter_context(tc.psum_pool(name="psum", bufs=1))
+
+        banks = [psum.tile([P, BANK], F32, name="bank%d" % i) for i in range(8)]
+
+        offs_t = lists.tile([P, S // 16], U16, name="offs_t")
+        pos1_t = lists.tile([P, M // 16], U16, name="pos1_t")
+        pos2_t = lists.tile([P, M // 16], U16, name="pos2_t")
+        tsc = stage.tile([P, T], U8, name="tsc", tag="slot_c", align_bytes=64)
+        wbs_raw = stage.tile([P, N], U8, name="wbs_raw", tag="slot_b", align_bytes=64)
+        was_raw = keep.tile([P, 2, N], U8, name="was_raw", align_bytes=64)
+        nc.gpsimd.memset(tsc[:, : T // 2].bitcast(I32), 0)
+        nc.vector.memset(tsc[:, T // 2 :].bitcast(I32), 0)
+        nc.vector.memset(wbs_raw[:].bitcast(I32), 0)
+        nc.vector.memset(was_raw[:].bitcast(I32), 0)
+        for q in range(4):
+            nc.gpsimd.dma_start(
+                tsc[32 * q : 32 * q + 8, :].bitcast(I32), tab_scales[:, 4 * q : 4 * q + 4, :].bitcast(I32)
+            )
+
+        nc.sync.dma_start(offs_t[:], offs)
+        wb_raw = keep.tile([P, 2, N], I32, name="wb_raw", align_bytes=64)
+        nc.sync.dma_start(wb_raw[:], wb_words.rearrange("a p c i -> p a (c i)").bitcast(I32))
+        wa_raw = stage.tile([P, 2, 2 * N], U8, name="wa_raw", tag="slot_a", align_bytes=64)
+        nc.sync.dma_start(wa_raw[:].bitcast(I32), wa_words.rearrange("a p c -> p a c").bitcast(I32))
+
+        tab = [stage.tile([P, T], I32, name="tab%d" % a, tag="slot_t%d" % a, align_bytes=64) for a in range(2)]
+        tab_src = [tab_words[a].rearrange("p t i -> p (t i)").bitcast(I32) for a in range(2)]
+        nc.sync.dma_start(tab[0][:, : T // 2], tab_src[0][:, : T // 2])
+        for q in range(4):
+            nc.sync.dma_start(
+                wbs_raw[32 * q : 32 * q + 8, :].bitcast(I32), wb_scales[:, 4 * q : 4 * q + 4, :].bitcast(I32)
+            )
+        nc.sync.dma_start(tab[0][:, T // 2 :], tab_src[0][:, T // 2 :])
+        for q in range(4):
+            nc.sync.dma_start(
+                was_raw[32 * q : 32 * q + 4, :, :].bitcast(I32),
+                wa_scales[:, 4 * q : 4 * q + 4, :].rearrange("a r n -> r a n").bitcast(I32),
+            )
+        nc.sync.dma_start(tab[1][:], tab_src[1])
+        nc.sync.dma_start(pos1_t[:], pos1)
+        nc.sync.dma_start(pos2_t[:], pos2)
+        ygain_t = keep.tile([P, PACK], F32, name="ygain_t")
+        nc.sync.dma_start(ygain_t[:], ygain.rearrange("(p t) -> p t", t=PACK))
+        hgain_t = keep.tile([P, 2, PACK], F32, name="hgain_t")
+        nc.sync.dma_start(hgain_t[:], hgain.rearrange("(b p t) -> p b t", b=2, t=PACK))
+        temp_t = keep.tile([P, PACK], F32, name="temp_t")
+        nc.sync.dma_start(temp_t[:], temp.rearrange("(p t) -> p t", t=PACK))
+        shift_t = keep.tile([P, PACK], F32, name="shift_t")
+        nc.sync.dma_start(shift_t[:], shift.rearrange("(p t) -> p t", t=PACK))
+
+        neg_ygain = keep.tile([P, PACK], F32, name="neg_ygain")
+        nc.scalar.mul(neg_ygain[:], ygain_t[:], -1.0)
+
+        wb_q = keep.tile([P, 2, N], I32, name="wb_q", align_bytes=64)
+        nc.vector.tensor_copy(
+            wb_q[:].rearrange("p a (t q) -> p a q t", t=PACK), wb_raw[:].rearrange("p a (q t) -> p a q t", t=PACK)
+        )
+        wa_q = keep.tile([P, 2, 2 * N], U8, name="wa_q", align_bytes=64)
+        for a in range(2):
+            nc.vector.tensor_copy(
+                wa_q[:, a, :].rearrange("p (t q e) -> p q t e", t=PACK, e=2),
+                wa_raw[:, a, :].rearrange("p (q t e) -> p q t e", t=PACK, e=2),
+            )
+        v_scales = keep.tile([P, S], U8, name="v_scales", align_bytes=64)
+        nc.vector.tensor_copy(v_scales[:], tsc[:].indirect(offs_t[:]))
+
+        wb_s = keep.tile([P, N], U8, name="wb_s", align_bytes=64)
+        nc.vector.tensor_copy(
+            wb_s[:].rearrange("p (t q) -> p q t", t=PACK), wbs_raw[:].rearrange("p (q t) -> p q t", t=PACK)
+        )
+
+        v_words = [keep.tile([P, S], U32, name="v_words%d" % a, align_bytes=64) for a in range(2)]
+        nc.vector.tensor_copy(v_words[0][:], tab[0][:].bitcast(U32).indirect(offs_t[:]))
+
+
+        def d_pass(a, half):
+            cols = slice(half * BANK, (half + 1) * BANK)
+            for t in range(PACK):
+                rows = slice(t * P, (t + 1) * P)
+                nc.tensor.matmul_mx(
+                    banks[PACK * half + t][:],
+                    lhsT=wb_q[:, a, rows].bitcast(FP8X4), lhsT_scale=wb_s[4 * a :, rows],
+                    rhs=v_words[a][:, cols].bitcast(FP8X4), rhs_scale=v_scales[4 * a :, cols],
+                    start=(a == 0), stop=(a == 1),
+                )
+
+        d_pass(0, 0)
+        d_pass(0, 1)
+        wa_s = stage.tile([P, 2, N], U8, name="wa_s", tag="slot_t0", align_bytes=64)
+        nc.vector.tensor_copy(
+            wa_s[:].rearrange("p a (t q) -> p a q t", t=PACK), was_raw[:].rearrange("p a (q t) -> p a q t", t=PACK)
+        )
+
+        w1_raw = {}
+        for (b, a), tag in zip([(0, 0), (0, 1), (1, 0), (1, 1)], ["slot_a", "slot_c", "slot_b", "slot_t1"]):
+            raw = stage.tile([P, PACK, PASS], F32, name="w1_raw%d%d" % (b, a), tag=tag, align_bytes=64)
+            nc.sync.dma_start(
+                raw[:],
+                w1[a * PASS : (a + 1) * PASS, b * PASS : (b + 1) * PASS].rearrange("(p j) c -> p j c", j=PACK),
+            )
+            w1_raw[(b, a)] = raw
+
+        d_rows = [keep.tile([P, S], F32, name="d_rows%d" % t) for t in range(PACK)]
+        for half in range(2):
+            cols = slice(half * BANK, (half + 1) * BANK)
+            entries = slice(half * BANK // 16, (half + 1) * BANK // 16)
+            nc.vector.tensor_copy(v_words[1][:, cols], tab[1][:].bitcast(U32).indirect(offs_t[:, entries]))
+            d_pass(1, half)
+            for t in range(PACK):
+                nc.scalar.copy(d_rows[t][:, cols], banks[PACK * half + t][:])
+
+        mat_t = stage.tile([P, PACK, M], F32, name="mat_t", tag="slot_a", align_bytes=64)
+        nc.sync.dma_start(mat_t[:], mat.rearrange("(p t) m -> p t m", t=PACK))
+
+        w1_q = {}
+        w1_s = {}
+        w1_bf = {}
+
+        def round_w1(b, a, on_scalar):
+            grouped = ring.tile([P, PACK * PASS], BF16, name="w1_bf", tag="w1_bf", bufs=2, align_bytes=64)
+            dst = grouped[:].rearrange("p (t m j) -> p m j t", t=PACK, j=PACK)
+            src = w1_raw[(b, a)][:].rearrange("p j (m t) -> p m j t", t=PACK)
+            if on_scalar:
+                nc.scalar.copy(dst, src)
+            else:
+                nc.vector.tensor_copy(dst, src)
+            w1_bf[(b, a)] = grouped
+
+        def quantise_w1(b, a):
+            codes = keep.tile([P, PASS], U32, name="w1_q%d%d" % (b, a), align_bytes=64)
+            scales = keep.tile([P, PASS], U8, name="w1_s%d%d" % (b, a), align_bytes=64)
+            nc.vector.quantize_mx(codes[:].bitcast(FP8X4), scales[:], w1_bf[(b, a)][:])
+            w1_q[(b, a)] = codes
+            w1_s[(b, a)] = scales
+
+        round_w1(0, 0, False)
+        quantise_w1(0, 0)
+        round_w1(0, 1, False)
+        quantise_w1(0, 1)
+        round_w1(1, 0, False)
+        quantise_w1(1, 0)
+
+        h_q = [keep.tile([P, S], U32, name="h_q%d" % b, align_bytes=64) for b in range(2)]
+        h_s = [keep.tile([P, S], U8, name="h_s%d" % b, align_bytes=64) for b in range(2)]
+        e_rows = [keep.tile([P, S], F32, name="e_rows%d" % t) for t in range(PACK)]
+        units = [(b, u) for b in range(2) for u in range(S // UNIT)]
+        tanh_of = {}
+        h_bf = {}
+
+        def tanh_unit(i):
+            b, u = units[i]
+            th = ring.tile([P, UNIT, PACK], F32, name="th", tag="th", bufs=4, align_bytes=64)
+            for c in range(UNIT // P):
+                bank = banks[(2 * i + c) % 4]
+                cols = slice(u * UNIT + c * P, u * UNIT + (c + 1) * P)
+                for t in range(PACK):
+                    rows = slice(t * P, (t + 1) * P)
+                    for a in range(2):
+                        nc.tensor.matmul_mx(
+                            bank[:, rows],
+                            lhsT=w1_q[(b, a)][:, rows].bitcast(FP8X4), lhsT_scale=w1_s[(b, a)][:, rows],
+                            rhs=v_words[a][:, cols].bitcast(FP8X4), rhs_scale=v_scales[4 * a :, cols],
+                            start=(a == 0), stop=(a == 1),
+                        )
+                nc.scalar.activation(
+                    th[:, c * P : (c + 1) * P, :], bank[:].rearrange("p (t n) -> p n t", t=PACK), ACT.Tanh
+                )
+            tanh_of[i] = th
+
+        def gain_unit(i):
+            b, u = units[i]
+            hb = ring.tile([P, UNIT, PACK], BF16, name="hb", tag="hb", bufs=3, align_bytes=64)
+            nc.vector.tensor_tensor(
+                hb[:], tanh_of[i][:], hgain_t[:, b : b + 1, :].to_broadcast([P, UNIT, PACK]), ALU.mult
+            )
+            h_bf[i] = hb
+
+        def quantise_unit(i):
+            b, u = units[i]
+            cols = slice(u * UNIT, (u + 1) * UNIT)
+            nc.vector.quantize_mx(
+                h_q[b][:, cols].bitcast(FP8X4), h_s[b][:, cols], h_bf[i][:].rearrange("p n t -> p (n t)")
+            )
+
+        def e_pass(b, u):
+            cols = slice(u * UNIT, (u + 1) * UNIT)
+            for t in range(PACK):
+                nc.tensor.matmul_mx(
+                    banks[4 + 2 * (u % 2) + t // 2][:, (t % 2) * UNIT : (t % 2 + 1) * UNIT],
+                    lhsT=wa_q[:, b, 2 * t * P : 2 * (t + 1) * P].bitcast(FP4X4),
+                    lhsT_scale=wa_s[:, b, t * P : (t + 1) * P],
+                    rhs=h_q[b][:, cols].bitcast(FP8X4), rhs_scale=h_s[b][:, cols],
+                    start=(b == 0 and t % 2 == 0), stop=(b == 1 and t % 2 == 1),
+                )
+
+        def e_out(u):
+            for t in range(PACK):
+                nc.scalar.copy(
+                    e_rows[t][:, u * UNIT : (u + 1) * UNIT],
+                    banks[4 + 2 * (u % 2) + t // 2][:, (t % 2) * UNIT : (t % 2 + 1) * UNIT],
+                )
+
+        matg = keep.tile([P, PACK, M], F32, name="matg")
+        per_block = S // UNIT
+
+        for i in range(len(units) + 2):
+            if i == per_block:
+                round_w1(1, 1, True)
+                quantise_w1(1, 1)
+            if i < len(units):
+                tanh_unit(i)
+                gain_unit(i)
+            if 0 < i <= len(units):
+                quantise_unit(i - 1)
+                if i - 1 >= per_block:
+                    e_pass(1, i - 1 - per_block)
+            if i - 2 >= per_block:
+                e_out(i - 2 - per_block)
+            if per_block <= i < len(units):
+                e_pass(0, i - per_block)
+            if i == per_block:
+                for t in range(PACK):
+                    nc.vector.tensor_scalar_mul(matg[:, t, :], mat_t[:, t, :], ygain_t[:, t : t + 1])
+
+        c_rows = []
+        for t in range(PACK):
+            c = ring.tile([P, M], F32, name="c_row", tag="th", bufs=4, align_bytes=64)
+            nc.vector.tensor_tensor(c[:], d_rows[t][:].indirect(pos2_t[:]), matg[:, t, :], ALU.mult)
+            c_rows.append(c)
+
+        y_q = keep.tile([P, M], U32, name="y_q", align_bytes=64)
+        y_s = keep.tile([P, M], U8, name="y_s", align_bytes=64)
+        out_rows = out_0.rearrange("(p t) m -> p t m", t=PACK)
+        out_words = out_1[0].rearrange("p m i -> p (m i)").bitcast(I32)
+        for half in range(M // HALF):
+            cols = slice(half * HALF, (half + 1) * HALF)
+            entries = slice(half * HALF // 16, (half + 1) * HALF // 16)
+            look = keep.tile([P, PACK, HALF], F32, name="look%d" % half)
+            y = keep.tile([P, PACK, HALF], F32, name="y%d" % half)
+            for t in range(PACK):
+                nc.scalar.activation(
+                    look[:, t, :], e_rows[t][:].indirect(pos1_t[:, entries]), ACT.Exp,
+                    bias=shift_t[:, t : t + 1], scale=temp_t[:, t : t + 1],
+                )
+                nc.vector.scalar_tensor_tensor(
+                    y[:, t, :], look[:, t, :], neg_ygain[:, t : t + 1], c_rows[t][:, cols], ALU.mult, ALU.add
+                )
+            nc.sync.dma_start(out_rows[:, :, cols], y[:])
+            y_bf = keep.tile([P, HALF * PACK], BF16, name="y_bf%d" % half, align_bytes=64)
+            nc.vector.tensor_copy(
+                y_bf[:].rearrange("p (c i t) -> p c t i", i=4, t=PACK),
+                y[:].rearrange("p t (c i) -> p c t i", i=4),
+            )
+            nc.vector.quantize_mx(y_q[:, cols].bitcast(FP8X4), y_s[:, cols], y_bf[:])
+            nc.sync.dma_start(out_words[:, cols], y_q[:, cols].bitcast(I32))
+        for q in range(4):
+            queue = nc.scalar if q % 2 == 0 else nc.sync
+            queue.dma_start(
+                out_2[0, 4 * q : 4 * q + 4, :].bitcast(I32), y_s[32 * q : 32 * q + 4, :].bitcast(I32)
+            )

@@ -89,20 +89,22 @@ def tile_list_tariff_spike_scores_kernel(
 
         wb_q = keep.tile([P, 2, N], I32, name="wb_q", align_bytes=64)
         nc.vector.tensor_copy(
-            wb_q[:].rearrange("p a (t q) -> p a q t", t=PACK), wb_raw[:].rearrange("p a (q t) -> p a q t", t=PACK)
+            wb_q[:].rearrange("p a (t g i) -> p a g t i", t=PACK, i=4),
+            wb_raw[:].rearrange("p a (g i t) -> p a g t i", t=PACK, i=4),
         )
         wa_q = keep.tile([P, 2, 2 * N], U8, name="wa_q", align_bytes=64)
         for a in range(2):
             nc.vector.tensor_copy(
-                wa_q[:, a, :].rearrange("p (t q e) -> p q t e", t=PACK, e=2),
-                wa_raw[:, a, :].rearrange("p (q t e) -> p q t e", t=PACK, e=2),
+                wa_q[:, a, :].rearrange("p (t g i e) -> p g t i e", t=PACK, i=8, e=2),
+                wa_raw[:, a, :].rearrange("p (g i t e) -> p g t i e", t=PACK, i=8, e=2),
             )
         v_scales = keep.tile([P, S], U8, name="v_scales", align_bytes=64)
         nc.vector.tensor_copy(v_scales[:], tsc[:].indirect(offs_t[:]))
 
         wb_s = keep.tile([P, N], U8, name="wb_s", align_bytes=64)
         nc.vector.tensor_copy(
-            wb_s[:].rearrange("p (t q) -> p q t", t=PACK), wbs_raw[:].rearrange("p (q t) -> p q t", t=PACK)
+            wb_s[:].rearrange("p (t g i) -> p g t i", t=PACK, i=16),
+            wbs_raw[:].rearrange("p (g i t) -> p g t i", t=PACK, i=16),
         )
 
         v_words = [keep.tile([P, S], U32, name="v_words%d" % a, align_bytes=64) for a in range(2)]
@@ -124,7 +126,8 @@ def tile_list_tariff_spike_scores_kernel(
         d_pass(0, 1)
         wa_s = stage.tile([P, 2, N], U8, name="wa_s", tag="slot_t0", align_bytes=64)
         nc.vector.tensor_copy(
-            wa_s[:].rearrange("p a (t q) -> p a q t", t=PACK), was_raw[:].rearrange("p a (q t) -> p a q t", t=PACK)
+            wa_s[:].rearrange("p a (t g i) -> p a g t i", t=PACK, i=16),
+            was_raw[:].rearrange("p a (g i t) -> p a g t i", t=PACK, i=16),
         )
 
         w1_raw = {}
@@ -154,8 +157,8 @@ def tile_list_tariff_spike_scores_kernel(
 
         def round_w1(b, a, on_scalar):
             grouped = ring.tile([P, PACK * PASS], BF16, name="w1_bf", tag="w1_bf", bufs=2, align_bytes=64)
-            dst = grouped[:].rearrange("p (t m j) -> p m j t", t=PACK, j=PACK)
-            src = w1_raw[(b, a)][:].rearrange("p j (m t) -> p m j t", t=PACK)
+            dst = grouped[:].rearrange("p (t m j) -> p m t j", t=PACK, j=PACK)
+            src = w1_raw[(b, a)][:].rearrange("p j (m t) -> p m t j", t=PACK)
             if on_scalar:
                 nc.scalar.copy(dst, src)
             else:
@@ -284,8 +287,8 @@ def tile_list_tariff_spike_scores_kernel(
             nc.sync.dma_start(out_rows[:, :, cols], y[:])
             y_bf = keep.tile([P, HALF * PACK], BF16, name="y_bf%d" % half, align_bytes=64)
             nc.vector.tensor_copy(
-                y_bf[:].rearrange("p (c i t) -> p c t i", i=4, t=PACK),
-                y[:].rearrange("p t (c i) -> p c t i", i=4),
+                y_bf[:].rearrange("p (m t) -> p m t", t=PACK),
+                y[:].rearrange("p t m -> p m t"),
             )
             nc.vector.quantize_mx(y_q[:, cols].bitcast(FP8X4), y_s[:, cols], y_bf[:])
             nc.sync.dma_start(out_words[:, cols], y_q[:, cols].bitcast(I32))

@@ -46,18 +46,20 @@ def tile_list_tariff_spike_scores_kernel(
         was_raw = keep.tile([P, 2, N], U8, name="was_raw", align_bytes=64)
         nc.gpsimd.memset(tsc[:, : T // 2].bitcast(I32), 0)
         nc.vector.memset(tsc[:, T // 2 :].bitcast(I32), 0)
-        nc.vector.memset(wbs_raw[:].bitcast(I32), 0)
-        nc.vector.memset(was_raw[:].bitcast(I32), 0)
-        for q in range(4):
-            nc.gpsimd.dma_start(
-                tsc[32 * q : 32 * q + 8, :].bitcast(I32), tab_scales[:, 4 * q : 4 * q + 4, :].bitcast(I32)
-            )
+        nc.gpsimd.memset(wbs_raw[:].bitcast(I32), 0)
+        nc.gpsimd.memset(was_raw[:].bitcast(I32), 0)
 
         nc.sync.dma_start(offs_t[:], offs)
+        nc.sync.dma_start(pos1_t[:], pos1)
+        nc.sync.dma_start(pos2_t[:], pos2)
         wb_raw = keep.tile([P, 2, N], I32, name="wb_raw", align_bytes=64)
         nc.sync.dma_start(wb_raw[:], wb_words.rearrange("a p c i -> p a (c i)").bitcast(I32))
         wa_raw = stage.tile([P, 2, 2 * N], U8, name="wa_raw", tag="slot_a", align_bytes=64)
         nc.sync.dma_start(wa_raw[:].bitcast(I32), wa_words.rearrange("a p c -> p a c").bitcast(I32))
+        for q in range(4):
+            nc.sync.dma_start(
+                tsc[32 * q : 32 * q + 8, :].bitcast(I32), tab_scales[:, 4 * q : 4 * q + 4, :].bitcast(I32)
+            )
 
         tab = [stage.tile([P, T], I32, name="tab%d" % a, tag="slot_t%d" % a, align_bytes=64) for a in range(2)]
         tab_src = [tab_words[a].rearrange("p t i -> p (t i)").bitcast(I32) for a in range(2)]
@@ -73,8 +75,6 @@ def tile_list_tariff_spike_scores_kernel(
                 wa_scales[:, 4 * q : 4 * q + 4, :].rearrange("a r n -> r a n").bitcast(I32),
             )
         nc.sync.dma_start(tab[1][:], tab_src[1])
-        nc.sync.dma_start(pos1_t[:], pos1)
-        nc.sync.dma_start(pos2_t[:], pos2)
         ygain_t = keep.tile([P, PACK], F32, name="ygain_t")
         nc.sync.dma_start(ygain_t[:], ygain.rearrange("(p t) -> p t", t=PACK))
         hgain_t = keep.tile([P, 2, PACK], F32, name="hgain_t")
@@ -89,26 +89,31 @@ def tile_list_tariff_spike_scores_kernel(
 
         wb_q = keep.tile([P, 2, N], I32, name="wb_q", align_bytes=64)
         nc.vector.tensor_copy(
-            wb_q[:].rearrange("p a (t g i) -> p a g t i", t=PACK, i=4),
-            wb_raw[:].rearrange("p a (g i t) -> p a g t i", t=PACK, i=4),
+            wb_q[:].rearrange("p a (t q) -> p a q t", t=PACK), wb_raw[:].rearrange("p a (q t) -> p a q t", t=PACK)
         )
         wa_q = keep.tile([P, 2, 2 * N], U8, name="wa_q", align_bytes=64)
         for a in range(2):
             nc.vector.tensor_copy(
-                wa_q[:, a, :].rearrange("p (t g i e) -> p g t i e", t=PACK, i=8, e=2),
-                wa_raw[:, a, :].rearrange("p (g i t e) -> p g t i e", t=PACK, i=8, e=2),
+                wa_q[:, a, :].rearrange("p (t q e) -> p q t e", t=PACK, e=2),
+                wa_raw[:, a, :].rearrange("p (q t e) -> p q t e", t=PACK, e=2),
             )
         v_scales = keep.tile([P, S], U8, name="v_scales", align_bytes=64)
         nc.vector.tensor_copy(v_scales[:], tsc[:].indirect(offs_t[:]))
 
-        wb_s = keep.tile([P, N], U8, name="wb_s", align_bytes=64)
-        nc.vector.tensor_copy(
-            wb_s[:].rearrange("p (t g i) -> p g t i", t=PACK, i=16),
-            wbs_raw[:].rearrange("p (g i t) -> p g t i", t=PACK, i=16),
-        )
 
         v_words = [keep.tile([P, S], U32, name="v_words%d" % a, align_bytes=64) for a in range(2)]
-        nc.vector.tensor_copy(v_words[0][:], tab[0][:].bitcast(U32).indirect(offs_t[:]))
+
+        def gather_words(a, half):
+            cols = slice(half * BANK, (half + 1) * BANK)
+            entries = slice(half * BANK // 16, (half + 1) * BANK // 16)
+            nc.vector.tensor_copy(v_words[a][:, cols], tab[a][:].bitcast(U32).indirect(offs_t[:, entries]))
+
+        wb_s = keep.tile([P, N], U8, name="wb_s", align_bytes=64)
+        nc.vector.tensor_copy(
+            wb_s[:].rearrange("p (t q) -> p q t", t=PACK), wbs_raw[:].rearrange("p (q t) -> p q t", t=PACK)
+        )
+        gather_words(0, 0)
+        gather_words(0, 1)
 
 
         def d_pass(a, half):
@@ -126,8 +131,7 @@ def tile_list_tariff_spike_scores_kernel(
         d_pass(0, 1)
         wa_s = stage.tile([P, 2, N], U8, name="wa_s", tag="slot_t0", align_bytes=64)
         nc.vector.tensor_copy(
-            wa_s[:].rearrange("p a (t g i) -> p a g t i", t=PACK, i=16),
-            was_raw[:].rearrange("p a (g i t) -> p a g t i", t=PACK, i=16),
+            wa_s[:].rearrange("p a (t q) -> p a q t", t=PACK), was_raw[:].rearrange("p a (q t) -> p a q t", t=PACK)
         )
 
         w1_raw = {}
@@ -142,8 +146,7 @@ def tile_list_tariff_spike_scores_kernel(
         d_rows = [keep.tile([P, S], F32, name="d_rows%d" % t) for t in range(PACK)]
         for half in range(2):
             cols = slice(half * BANK, (half + 1) * BANK)
-            entries = slice(half * BANK // 16, (half + 1) * BANK // 16)
-            nc.vector.tensor_copy(v_words[1][:, cols], tab[1][:].bitcast(U32).indirect(offs_t[:, entries]))
+            gather_words(1, half)
             d_pass(1, half)
             for t in range(PACK):
                 nc.scalar.copy(d_rows[t][:, cols], banks[PACK * half + t][:])
@@ -157,18 +160,25 @@ def tile_list_tariff_spike_scores_kernel(
 
         def round_w1(b, a, on_scalar):
             grouped = ring.tile([P, PACK * PASS], BF16, name="w1_bf", tag="w1_bf", bufs=2, align_bytes=64)
-            dst = grouped[:].rearrange("p (t m j) -> p m t j", t=PACK, j=PACK)
-            src = w1_raw[(b, a)][:].rearrange("p j (m t) -> p m t j", t=PACK)
-            if on_scalar:
-                nc.scalar.copy(dst, src)
-            else:
-                nc.vector.tensor_copy(dst, src)
+            dst = grouped[:].rearrange("p (t m j) -> p m j t", t=PACK, j=PACK)
+            src = w1_raw[(b, a)][:].rearrange("p j (m t) -> p m j t", t=PACK)
+            for pair in range(2):
+                ts = slice(2 * pair, 2 * pair + 2)
+                if on_scalar:
+                    nc.scalar.copy(dst[:, :, :, ts], src[:, :, :, ts])
+                else:
+                    nc.vector.tensor_copy(dst[:, :, :, ts], src[:, :, :, ts])
             w1_bf[(b, a)] = grouped
 
         def quantise_w1(b, a):
             codes = keep.tile([P, PASS], U32, name="w1_q%d%d" % (b, a), align_bytes=64)
             scales = keep.tile([P, PASS], U8, name="w1_s%d%d" % (b, a), align_bytes=64)
-            nc.vector.quantize_mx(codes[:].bitcast(FP8X4), scales[:], w1_bf[(b, a)][:])
+            for pair in range(2):
+                cols = slice(pair * PASS // 2, (pair + 1) * PASS // 2)
+                nc.vector.quantize_mx(
+                    codes[:, cols].bitcast(FP8X4), scales[:, cols],
+                    w1_bf[(b, a)][:, PACK * cols.start : PACK * cols.stop],
+                )
             w1_q[(b, a)] = codes
             w1_s[(b, a)] = scales
 
@@ -188,7 +198,10 @@ def tile_list_tariff_spike_scores_kernel(
 
         def tanh_unit(i):
             b, u = units[i]
-            th = ring.tile([P, UNIT, PACK], F32, name="th", tag="th", bufs=4, align_bytes=64)
+            if i == len(units) - 1:
+                th = ring.tile([P, UNIT, PACK], F32, name="th_last", tag="th_last", align_bytes=64)
+            else:
+                th = ring.tile([P, UNIT, PACK], F32, name="th", tag="th", bufs=4, align_bytes=64)
             for c in range(UNIT // P):
                 bank = banks[(2 * i + c) % 4]
                 cols = slice(u * UNIT + c * P, u * UNIT + (c + 1) * P)
@@ -261,36 +274,43 @@ def tile_list_tariff_spike_scores_kernel(
                 for t in range(PACK):
                     nc.vector.tensor_scalar_mul(matg[:, t, :], mat_t[:, t, :], ygain_t[:, t : t + 1])
 
-        c_rows = []
-        for t in range(PACK):
-            c = ring.tile([P, M], F32, name="c_row", tag="th", bufs=4, align_bytes=64)
-            nc.vector.tensor_tensor(c[:], d_rows[t][:].indirect(pos2_t[:]), matg[:, t, :], ALU.mult)
-            c_rows.append(c)
-
         y_q = keep.tile([P, M], U32, name="y_q", align_bytes=64)
         y_s = keep.tile([P, M], U8, name="y_s", align_bytes=64)
         out_rows = out_0.rearrange("(p t) m -> p t m", t=PACK)
         out_words = out_1[0].rearrange("p m i -> p (m i)").bitcast(I32)
+        y = []
         for half in range(M // HALF):
             cols = slice(half * HALF, (half + 1) * HALF)
             entries = slice(half * HALF // 16, (half + 1) * HALF // 16)
-            look = keep.tile([P, PACK, HALF], F32, name="look%d" % half)
-            y = keep.tile([P, PACK, HALF], F32, name="y%d" % half)
+            picked = ring.tile([P, PACK, HALF], F32, name="picked", tag=["th_last", "look0"][half], align_bytes=64)
+            for t in range(PACK):
+                nc.vector.tensor_tensor(
+                    picked[:, t, :], d_rows[t][:].indirect(pos2_t[:, entries]), matg[:, t, cols], ALU.mult
+                )
+            look = ring.tile([P, PACK, HALF], F32, name="look", tag="look%d" % half, align_bytes=64)
+            y_half = keep.tile([P, PACK, HALF], F32, name="y%d" % half)
             for t in range(PACK):
                 nc.scalar.activation(
                     look[:, t, :], e_rows[t][:].indirect(pos1_t[:, entries]), ACT.Exp,
                     bias=shift_t[:, t : t + 1], scale=temp_t[:, t : t + 1],
                 )
                 nc.vector.scalar_tensor_tensor(
-                    y[:, t, :], look[:, t, :], neg_ygain[:, t : t + 1], c_rows[t][:, cols], ALU.mult, ALU.add
+                    y_half[:, t, :], look[:, t, :], neg_ygain[:, t : t + 1], picked[:, t, :], ALU.mult, ALU.add
                 )
-            nc.sync.dma_start(out_rows[:, :, cols], y[:])
-            y_bf = keep.tile([P, HALF * PACK], BF16, name="y_bf%d" % half, align_bytes=64)
-            nc.vector.tensor_copy(
-                y_bf[:].rearrange("p (m t) -> p m t", t=PACK),
-                y[:].rearrange("p t m -> p m t"),
-            )
-            nc.vector.quantize_mx(y_q[:, cols].bitcast(FP8X4), y_s[:, cols], y_bf[:])
+                if t % 2 == 1:
+                    nc.sync.dma_start(out_rows[:, t - 1 : t + 1, cols], y_half[:, t - 1 : t + 1, :])
+            y.append(y_half)
+
+        for half in range(M // HALF):
+            cols = slice(half * HALF, (half + 1) * HALF)
+            y_bf = keep.tile([P, HALF, PACK], BF16, name="y_bf%d" % half, align_bytes=64)
+            src = y[half][:].rearrange("p t (c i) -> p c t i", i=4)
+            dst = y_bf[:].rearrange("p (c i) t -> p c t i", i=4)
+            on_vector = half * HALF // 8
+            if on_vector > 0:
+                nc.vector.tensor_copy(dst[:, :on_vector], src[:, :on_vector])
+            nc.scalar.copy(dst[:, on_vector:], src[:, on_vector:])
+            nc.vector.quantize_mx(y_q[:, cols].bitcast(FP8X4), y_s[:, cols], y_bf[:].rearrange("p m t -> p (m t)"))
             nc.sync.dma_start(out_words[:, cols], y_q[:, cols].bitcast(I32))
         for q in range(4):
             queue = nc.scalar if q % 2 == 0 else nc.sync

@@ -54,27 +54,27 @@ def tile_list_tariff_spike_scores_kernel(
         nc.sync.dma_start(pos2_t[:], pos2)
         wb_raw = keep.tile([P, 2, N], I32, name="wb_raw", align_bytes=64)
         nc.sync.dma_start(wb_raw[:], wb_words.rearrange("a p c i -> p a (c i)").bitcast(I32))
-        wa_raw = stage.tile([P, 2, 2 * N], U8, name="wa_raw", tag="slot_a", align_bytes=64)
+        wa_raw = keep.tile([P, 2, N], U16, name="wa_raw", align_bytes=64)
         nc.sync.dma_start(wa_raw[:].bitcast(I32), wa_words.rearrange("a p c -> p a c").bitcast(I32))
-        for q in range(4):
-            nc.sync.dma_start(
-                tsc[32 * q : 32 * q + 8, :].bitcast(I32), tab_scales[:, 4 * q : 4 * q + 4, :].bitcast(I32)
-            )
-
         tab = [stage.tile([P, T], I32, name="tab%d" % a, tag="slot_t%d" % a, align_bytes=64) for a in range(2)]
         tab_src = [tab_words[a].rearrange("p t i -> p (t i)").bitcast(I32) for a in range(2)]
         nc.sync.dma_start(tab[0][:, : T // 2], tab_src[0][:, : T // 2])
         for q in range(4):
             nc.sync.dma_start(
-                wbs_raw[32 * q : 32 * q + 8, :].bitcast(I32), wb_scales[:, 4 * q : 4 * q + 4, :].bitcast(I32)
+                tsc[32 * q : 32 * q + 8, :].bitcast(I32), tab_scales[:, 4 * q : 4 * q + 4, :].bitcast(I32)
             )
         nc.sync.dma_start(tab[0][:, T // 2 :], tab_src[0][:, T // 2 :])
+        for q in range(4):
+            nc.sync.dma_start(
+                wbs_raw[32 * q : 32 * q + 8, :].bitcast(I32), wb_scales[:, 4 * q : 4 * q + 4, :].bitcast(I32)
+            )
+        nc.sync.dma_start(tab[1][:, : T // 2], tab_src[1][:, : T // 2])
         for q in range(4):
             nc.sync.dma_start(
                 was_raw[32 * q : 32 * q + 4, :, :].bitcast(I32),
                 wa_scales[:, 4 * q : 4 * q + 4, :].rearrange("a r n -> r a n").bitcast(I32),
             )
-        nc.sync.dma_start(tab[1][:], tab_src[1])
+        nc.sync.dma_start(tab[1][:, T // 2 :], tab_src[1][:, T // 2 :])
         ygain_t = keep.tile([P, PACK], F32, name="ygain_t")
         nc.sync.dma_start(ygain_t[:], ygain.rearrange("(p t) -> p t", t=PACK))
         hgain_t = keep.tile([P, 2, PACK], F32, name="hgain_t")
@@ -84,6 +84,12 @@ def tile_list_tariff_spike_scores_kernel(
         shift_t = keep.tile([P, PACK], F32, name="shift_t")
         nc.sync.dma_start(shift_t[:], shift.rearrange("(p t) -> p t", t=PACK))
 
+        wa_q = keep.tile([P, 2, N], U16, name="wa_q", align_bytes=64)
+        nc.scalar.copy(
+            wa_q[:].rearrange("p a (t g i) -> p a g t i", t=PACK, i=8),
+            wa_raw[:].rearrange("p a (g i t) -> p a g t i", t=PACK, i=8),
+        )
+
         neg_ygain = keep.tile([P, PACK], F32, name="neg_ygain")
         nc.scalar.mul(neg_ygain[:], ygain_t[:], -1.0)
 
@@ -91,12 +97,6 @@ def tile_list_tariff_spike_scores_kernel(
         nc.vector.tensor_copy(
             wb_q[:].rearrange("p a (t q) -> p a q t", t=PACK), wb_raw[:].rearrange("p a (q t) -> p a q t", t=PACK)
         )
-        wa_q = keep.tile([P, 2, 2 * N], U8, name="wa_q", align_bytes=64)
-        for a in range(2):
-            nc.vector.tensor_copy(
-                wa_q[:, a, :].rearrange("p (t q e) -> p q t e", t=PACK, e=2),
-                wa_raw[:, a, :].rearrange("p (q t e) -> p q t e", t=PACK, e=2),
-            )
         v_scales = keep.tile([P, S], U8, name="v_scales", align_bytes=64)
         nc.vector.tensor_copy(v_scales[:], tsc[:].indirect(offs_t[:]))
 
@@ -135,13 +135,19 @@ def tile_list_tariff_spike_scores_kernel(
         )
 
         w1_raw = {}
-        for (b, a), tag in zip([(0, 0), (0, 1), (1, 0), (1, 1)], ["slot_a", "slot_c", "slot_b", "slot_t1"]):
+
+        def load_w1(b, a, tag, pieces):
             raw = stage.tile([P, PACK, PASS], F32, name="w1_raw%d%d" % (b, a), tag=tag, align_bytes=64)
-            nc.sync.dma_start(
-                raw[:],
-                w1[a * PASS : (a + 1) * PASS, b * PASS : (b + 1) * PASS].rearrange("(p j) c -> p j c", j=PACK),
-            )
+            src = w1[a * PASS : (a + 1) * PASS, b * PASS : (b + 1) * PASS].rearrange("(p j) c -> p j c", j=PACK)
+            for piece in range(pieces):
+                cols = slice(piece * PASS // pieces, (piece + 1) * PASS // pieces)
+                nc.sync.dma_start(raw[:, :, cols], src[:, :, cols])
             w1_raw[(b, a)] = raw
+
+        load_w1(0, 0, "slot_a", 1)
+        load_w1(0, 1, "slot_c", 2)
+        load_w1(1, 0, "slot_b", 1)
+        load_w1(1, 1, "slot_t1", 1)
 
         d_rows = [keep.tile([P, S], F32, name="d_rows%d" % t) for t in range(PACK)]
         for half in range(2):
@@ -158,16 +164,18 @@ def tile_list_tariff_spike_scores_kernel(
         w1_s = {}
         w1_bf = {}
 
-        def round_w1(b, a, on_scalar):
+        def round_w1(b, a, on_scalar, pieces):
             grouped = ring.tile([P, PACK * PASS], BF16, name="w1_bf", tag="w1_bf", bufs=2, align_bytes=64)
             dst = grouped[:].rearrange("p (t m j) -> p m j t", t=PACK, j=PACK)
             src = w1_raw[(b, a)][:].rearrange("p j (m t) -> p m j t", t=PACK)
-            for pair in range(2):
-                ts = slice(2 * pair, 2 * pair + 2)
-                if on_scalar:
-                    nc.scalar.copy(dst[:, :, :, ts], src[:, :, :, ts])
-                else:
-                    nc.vector.tensor_copy(dst[:, :, :, ts], src[:, :, :, ts])
+            for piece in range(pieces):
+                ms = slice(piece * P // pieces, (piece + 1) * P // pieces)
+                for pair in range(2):
+                    ts = slice(2 * pair, 2 * pair + 2)
+                    if on_scalar:
+                        nc.scalar.copy(dst[:, ms, :, ts], src[:, ms, :, ts])
+                    else:
+                        nc.vector.tensor_copy(dst[:, ms, :, ts], src[:, ms, :, ts])
             w1_bf[(b, a)] = grouped
 
         def quantise_w1(b, a):
@@ -182,11 +190,11 @@ def tile_list_tariff_spike_scores_kernel(
             w1_q[(b, a)] = codes
             w1_s[(b, a)] = scales
 
-        round_w1(0, 0, False)
+        round_w1(0, 0, False, 1)
         quantise_w1(0, 0)
-        round_w1(0, 1, False)
+        round_w1(0, 1, False, 2)
         quantise_w1(0, 1)
-        round_w1(1, 0, False)
+        round_w1(1, 0, False, 1)
         quantise_w1(1, 0)
 
         h_q = [keep.tile([P, S], U32, name="h_q%d" % b, align_bytes=64) for b in range(2)]
@@ -205,14 +213,14 @@ def tile_list_tariff_spike_scores_kernel(
             for c in range(UNIT // P):
                 bank = banks[(2 * i + c) % 4]
                 cols = slice(u * UNIT + c * P, u * UNIT + (c + 1) * P)
-                for t in range(PACK):
-                    rows = slice(t * P, (t + 1) * P)
-                    for a in range(2):
+                for a in range(2):
+                    for t in range(PACK):
+                        rows = slice(t * P, (t + 1) * P)
                         nc.tensor.matmul_mx(
                             bank[:, rows],
                             lhsT=w1_q[(b, a)][:, rows].bitcast(FP8X4), lhsT_scale=w1_s[(b, a)][:, rows],
                             rhs=v_words[a][:, cols].bitcast(FP8X4), rhs_scale=v_scales[4 * a :, cols],
-                            start=(a == 0), stop=(a == 1),
+                            start=(a == 0 and t == 0), stop=(a == 1 and t == PACK - 1),
                         )
                 nc.scalar.activation(
                     th[:, c * P : (c + 1) * P, :], bank[:].rearrange("p (t n) -> p n t", t=PACK), ACT.Tanh
@@ -234,45 +242,66 @@ def tile_list_tariff_spike_scores_kernel(
                 h_q[b][:, cols].bitcast(FP8X4), h_s[b][:, cols], h_bf[i][:].rearrange("p n t -> p (n t)")
             )
 
-        def e_pass(b, u):
-            cols = slice(u * UNIT, (u + 1) * UNIT)
+        def e_pass(out, t, b, cols, start, stop):
+            nc.tensor.matmul_mx(
+                out,
+                lhsT=wa_q[:, b, t * P : (t + 1) * P].bitcast(U8).bitcast(FP4X4),
+                lhsT_scale=wa_s[:, b, t * P : (t + 1) * P],
+                rhs=h_q[b][:, cols].bitcast(FP8X4), rhs_scale=h_s[b][:, cols],
+                start=start, stop=stop,
+            )
+
+        def e_place(u, t):
+            if u < 2:
+                return banks[4 + 2 * u + t // 2][:, (t % 2) * UNIT : (t % 2 + 1) * UNIT]
+            return banks[t][:, (u - 2) * UNIT : (u - 1) * UNIT]
+
+        def e_first(u):
             for t in range(PACK):
-                nc.tensor.matmul_mx(
-                    banks[4 + 2 * (u % 2) + t // 2][:, (t % 2) * UNIT : (t % 2 + 1) * UNIT],
-                    lhsT=wa_q[:, b, 2 * t * P : 2 * (t + 1) * P].bitcast(FP4X4),
-                    lhsT_scale=wa_s[:, b, t * P : (t + 1) * P],
-                    rhs=h_q[b][:, cols].bitcast(FP8X4), rhs_scale=h_s[b][:, cols],
-                    start=(b == 0 and t % 2 == 0), stop=(b == 1 and t % 2 == 1),
-                )
+                if u < 2:
+                    e_pass(e_place(u, t), t, 0, slice(u * UNIT, (u + 1) * UNIT), t % 2 == 0, False)
+                else:
+                    e_pass(banks[t][:], t, 0, slice(BANK, S), True, False)
+
+        def e_second(u):
+            for t in range(PACK):
+                stop = t % 2 == 1 if u < 2 else u == 3
+                e_pass(e_place(u, t), t, 1, slice(u * UNIT, (u + 1) * UNIT), False, stop)
 
         def e_out(u):
             for t in range(PACK):
-                nc.scalar.copy(
-                    e_rows[t][:, u * UNIT : (u + 1) * UNIT],
-                    banks[4 + 2 * (u % 2) + t // 2][:, (t % 2) * UNIT : (t % 2 + 1) * UNIT],
-                )
+                if u < 2:
+                    nc.scalar.copy(e_rows[t][:, u * UNIT : (u + 1) * UNIT], e_place(u, t))
+                elif t < PACK - 1:
+                    nc.scalar.copy(e_rows[t][:, BANK:], banks[t][:])
+                else:
+                    nc.vector.tensor_copy(e_rows[t][:, BANK:], banks[t][:])
 
         matg = keep.tile([P, PACK, M], F32, name="matg")
         per_block = S // UNIT
 
-        for i in range(len(units) + 2):
+        for i in range(len(units)):
             if i == per_block:
-                round_w1(1, 1, True)
+                round_w1(1, 1, True, 1)
                 quantise_w1(1, 1)
-            if i < len(units):
-                tanh_unit(i)
-                gain_unit(i)
-            if 0 < i <= len(units):
+            tanh_unit(i)
+            gain_unit(i)
+            if i > 0:
                 quantise_unit(i - 1)
-                if i - 1 >= per_block:
-                    e_pass(1, i - 1 - per_block)
-            if i - 2 >= per_block:
-                e_out(i - 2 - per_block)
-            if per_block <= i < len(units):
-                e_pass(0, i - per_block)
             if i == per_block:
+                e_first(0)
+                e_first(1)
                 for t in range(PACK):
                     nc.vector.tensor_scalar_mul(matg[:, t, :], mat_t[:, t, :], ygain_t[:, t : t + 1])
+        quantise_unit(len(units) - 1)
+        e_second(0)
+        e_out(0)
+        e_second(1)
+        e_out(1)
+        e_first(2)
+        e_second(2)
+        e_second(3)
+        e_out(2)
 
         y_q = keep.tile([P, M], U32, name="y_q", align_bytes=64)
         y_s = keep.tile([P, M], U8, name="y_s", align_bytes=64)
@@ -306,10 +335,11 @@ def tile_list_tariff_spike_scores_kernel(
             y_bf = keep.tile([P, HALF, PACK], BF16, name="y_bf%d" % half, align_bytes=64)
             src = y[half][:].rearrange("p t (c i) -> p c t i", i=4)
             dst = y_bf[:].rearrange("p (c i) t -> p c t i", i=4)
-            on_vector = half * HALF // 8
-            if on_vector > 0:
-                nc.vector.tensor_copy(dst[:, :on_vector], src[:, :on_vector])
-            nc.scalar.copy(dst[:, on_vector:], src[:, on_vector:])
+            if half == 0:
+                nc.vector.tensor_copy(dst, src)
+            else:
+                nc.vector.tensor_copy(dst[:, : HALF // 8], src[:, : HALF // 8])
+                nc.scalar.copy(dst[:, HALF // 8 :], src[:, HALF // 8 :])
             nc.vector.quantize_mx(y_q[:, cols].bitcast(FP8X4), y_s[:, cols], y_bf[:].rearrange("p m t -> p (m t)"))
             nc.sync.dma_start(out_words[:, cols], y_q[:, cols].bitcast(I32))
         for q in range(4):

@@ -19,9 +19,14 @@ ALU = mybir.AluOpType
 P = 128
 PACK = 4
 PASS = P * PACK
+PASSES = 2
+QUADRANTS = 4
+PER_COLUMN = 16
 BANK = 512
+STAGE1_BANKS = 4
 UNIT = 256
-HALF = 256
+UNITS = S // UNIT
+HALF = M // 2
 
 
 def tile_list_tariff_spike_scores_kernel(
@@ -38,83 +43,91 @@ def tile_list_tariff_spike_scores_kernel(
 
         banks = [psum.tile([P, BANK], F32, name="bank%d" % i) for i in range(8)]
 
-        offs_t = lists.tile([P, S // 16], U16, name="offs_t")
-        pos1_t = lists.tile([P, M // 16], U16, name="pos1_t")
-        pos2_t = lists.tile([P, M // 16], U16, name="pos2_t")
-        tsc = stage.tile([P, T], U8, name="tsc", tag="slot_c", align_bytes=64)
-        wbs_raw = stage.tile([P, N], U8, name="wbs_raw", tag="slot_b", align_bytes=64)
-        was_raw = keep.tile([P, 2, N], U8, name="was_raw", align_bytes=64)
-        nc.gpsimd.memset(tsc[:, : T // 2].bitcast(I32), 0)
-        nc.vector.memset(tsc[:, T // 2 :].bitcast(I32), 0)
-        nc.gpsimd.memset(wbs_raw[:].bitcast(I32), 0)
-        nc.gpsimd.memset(was_raw[:].bitcast(I32), 0)
+        def entries_of(cols):
+            return slice(cols.start // PER_COLUMN, cols.stop // PER_COLUMN)
+
+        offs_t = lists.tile([P, S // PER_COLUMN], U16, name="offs_t")
+        pos1_t = lists.tile([P, M // PER_COLUMN], U16, name="pos1_t")
+        pos2_t = lists.tile([P, M // PER_COLUMN], U16, name="pos2_t")
+
+        tab_scale_rows = stage.tile([P, T], U8, name="tab_scale_rows", tag="slot_c", align_bytes=64)
+        wb_scale_rows = stage.tile([P, N], U8, name="wb_scale_rows", tag="slot_b", align_bytes=64)
+        wa_scale_rows = keep.tile([P, PASSES, N], U8, name="wa_scale_rows", align_bytes=64)
+        nc.gpsimd.memset(tab_scale_rows[:, : T // 2].bitcast(I32), 0)
+        nc.vector.memset(tab_scale_rows[:, T // 2 :].bitcast(I32), 0)
+        nc.gpsimd.memset(wb_scale_rows[:].bitcast(I32), 0)
+        nc.gpsimd.memset(wa_scale_rows[:].bitcast(I32), 0)
 
         nc.sync.dma_start(offs_t[:], offs)
         nc.sync.dma_start(pos1_t[:], pos1)
         nc.sync.dma_start(pos2_t[:], pos2)
-        wb_raw = keep.tile([P, 2, N], I32, name="wb_raw", align_bytes=64)
+        wb_raw = keep.tile([P, PASSES, N], I32, name="wb_raw", align_bytes=64)
         nc.sync.dma_start(wb_raw[:], wb_words.rearrange("a p c i -> p a (c i)").bitcast(I32))
-        wa_raw = keep.tile([P, 2, N], U16, name="wa_raw", align_bytes=64)
+        wa_raw = keep.tile([P, PASSES, N], U16, name="wa_raw", align_bytes=64)
         nc.sync.dma_start(wa_raw[:].bitcast(I32), wa_words.rearrange("a p c -> p a c").bitcast(I32))
-        tab = [stage.tile([P, T], I32, name="tab%d" % a, tag="slot_t%d" % a, align_bytes=64) for a in range(2)]
-        tab_src = [tab_words[a].rearrange("p t i -> p (t i)").bitcast(I32) for a in range(2)]
+
+        tab = [stage.tile([P, T], I32, name="tab%d" % a, tag="slot_t%d" % a, align_bytes=64) for a in range(PASSES)]
+        tab_src = [tab_words[a].rearrange("p t i -> p (t i)").bitcast(I32) for a in range(PASSES)]
         nc.sync.dma_start(tab[0][:, : T // 2], tab_src[0][:, : T // 2])
-        for q in range(4):
+        for q in range(QUADRANTS):
             nc.sync.dma_start(
-                tsc[32 * q : 32 * q + 8, :].bitcast(I32), tab_scales[:, 4 * q : 4 * q + 4, :].bitcast(I32)
+                tab_scale_rows[32 * q : 32 * q + 8, :].bitcast(I32),
+                tab_scales[:, 4 * q : 4 * q + 4, :].bitcast(I32),
             )
         nc.sync.dma_start(tab[0][:, T // 2 :], tab_src[0][:, T // 2 :])
-        for q in range(4):
+        for q in range(QUADRANTS):
             nc.sync.dma_start(
-                wbs_raw[32 * q : 32 * q + 8, :].bitcast(I32), wb_scales[:, 4 * q : 4 * q + 4, :].bitcast(I32)
+                wb_scale_rows[32 * q : 32 * q + 8, :].bitcast(I32),
+                wb_scales[:, 4 * q : 4 * q + 4, :].bitcast(I32),
             )
         nc.sync.dma_start(tab[1][:, : T // 2], tab_src[1][:, : T // 2])
-        for q in range(4):
+        for q in range(QUADRANTS):
             nc.sync.dma_start(
-                was_raw[32 * q : 32 * q + 4, :, :].bitcast(I32),
+                wa_scale_rows[32 * q : 32 * q + 4, :, :].bitcast(I32),
                 wa_scales[:, 4 * q : 4 * q + 4, :].rearrange("a r n -> r a n").bitcast(I32),
             )
         nc.sync.dma_start(tab[1][:, T // 2 :], tab_src[1][:, T // 2 :])
         ygain_t = keep.tile([P, PACK], F32, name="ygain_t")
         nc.sync.dma_start(ygain_t[:], ygain.rearrange("(p t) -> p t", t=PACK))
-        hgain_t = keep.tile([P, 2, PACK], F32, name="hgain_t")
-        nc.sync.dma_start(hgain_t[:], hgain.rearrange("(b p t) -> p b t", b=2, t=PACK))
+        hgain_t = keep.tile([P, PASSES, PACK], F32, name="hgain_t")
+        nc.sync.dma_start(hgain_t[:], hgain.rearrange("(b p t) -> p b t", b=PASSES, t=PACK))
         temp_t = keep.tile([P, PACK], F32, name="temp_t")
         nc.sync.dma_start(temp_t[:], temp.rearrange("(p t) -> p t", t=PACK))
         shift_t = keep.tile([P, PACK], F32, name="shift_t")
         nc.sync.dma_start(shift_t[:], shift.rearrange("(p t) -> p t", t=PACK))
 
-        wa_q = keep.tile([P, 2, N], U16, name="wa_q", align_bytes=64)
+        wa_codes = keep.tile([P, PASSES, N], U16, name="wa_codes", align_bytes=64)
         nc.scalar.copy(
-            wa_q[:].rearrange("p a (t g i) -> p a g t i", t=PACK, i=8),
+            wa_codes[:].rearrange("p a (t g i) -> p a g t i", t=PACK, i=8),
             wa_raw[:].rearrange("p a (g i t) -> p a g t i", t=PACK, i=8),
         )
 
         neg_ygain = keep.tile([P, PACK], F32, name="neg_ygain")
         nc.scalar.mul(neg_ygain[:], ygain_t[:], -1.0)
 
-        wb_q = keep.tile([P, 2, N], I32, name="wb_q", align_bytes=64)
+        wb_codes = keep.tile([P, PASSES, N], I32, name="wb_codes", align_bytes=64)
         nc.vector.tensor_copy(
-            wb_q[:].rearrange("p a (t q) -> p a q t", t=PACK), wb_raw[:].rearrange("p a (q t) -> p a q t", t=PACK)
+            wb_codes[:].rearrange("p a (t m) -> p a m t", t=PACK),
+            wb_raw[:].rearrange("p a (m t) -> p a m t", t=PACK),
         )
-        v_scales = keep.tile([P, S], U8, name="v_scales", align_bytes=64)
-        nc.vector.tensor_copy(v_scales[:], tsc[:].indirect(offs_t[:]))
+        v_scale = keep.tile([P, S], U8, name="v_scale", align_bytes=64)
+        nc.vector.tensor_copy(v_scale[:], tab_scale_rows[:].indirect(offs_t[:]))
 
-
-        v_words = [keep.tile([P, S], U32, name="v_words%d" % a, align_bytes=64) for a in range(2)]
+        v_codes = [keep.tile([P, S], U32, name="v_codes%d" % a, align_bytes=64) for a in range(PASSES)]
 
         def gather_words(a, half):
             cols = slice(half * BANK, (half + 1) * BANK)
-            entries = slice(half * BANK // 16, (half + 1) * BANK // 16)
-            nc.vector.tensor_copy(v_words[a][:, cols], tab[a][:].bitcast(U32).indirect(offs_t[:, entries]))
+            nc.vector.tensor_copy(
+                v_codes[a][:, cols], tab[a][:].bitcast(U32).indirect(offs_t[:, entries_of(cols)])
+            )
 
-        wb_s = keep.tile([P, N], U8, name="wb_s", align_bytes=64)
+        wb_scale = keep.tile([P, N], U8, name="wb_scale", align_bytes=64)
         nc.vector.tensor_copy(
-            wb_s[:].rearrange("p (t q) -> p q t", t=PACK), wbs_raw[:].rearrange("p (q t) -> p q t", t=PACK)
+            wb_scale[:].rearrange("p (t m) -> p m t", t=PACK),
+            wb_scale_rows[:].rearrange("p (m t) -> p m t", t=PACK),
         )
         gather_words(0, 0)
         gather_words(0, 1)
-
 
         def d_pass(a, half):
             cols = slice(half * BANK, (half + 1) * BANK)
@@ -122,16 +135,17 @@ def tile_list_tariff_spike_scores_kernel(
                 rows = slice(t * P, (t + 1) * P)
                 nc.tensor.matmul_mx(
                     banks[PACK * half + t][:],
-                    lhsT=wb_q[:, a, rows].bitcast(FP8X4), lhsT_scale=wb_s[4 * a :, rows],
-                    rhs=v_words[a][:, cols].bitcast(FP8X4), rhs_scale=v_scales[4 * a :, cols],
-                    start=(a == 0), stop=(a == 1),
+                    lhsT=wb_codes[:, a, rows].bitcast(FP8X4), lhsT_scale=wb_scale[4 * a :, rows],
+                    rhs=v_codes[a][:, cols].bitcast(FP8X4), rhs_scale=v_scale[4 * a :, cols],
+                    start=(a == 0), stop=(a == PASSES - 1),
                 )
 
         d_pass(0, 0)
         d_pass(0, 1)
-        wa_s = stage.tile([P, 2, N], U8, name="wa_s", tag="slot_t0", align_bytes=64)
+        wa_scale = stage.tile([P, PASSES, N], U8, name="wa_scale", tag="slot_t0", align_bytes=64)
         nc.vector.tensor_copy(
-            wa_s[:].rearrange("p a (t q) -> p a q t", t=PACK), was_raw[:].rearrange("p a (q t) -> p a q t", t=PACK)
+            wa_scale[:].rearrange("p a (t m) -> p a m t", t=PACK),
+            wa_scale_rows[:].rearrange("p a (m t) -> p a m t", t=PACK),
         )
 
         w1_raw = {}
@@ -150,7 +164,7 @@ def tile_list_tariff_spike_scores_kernel(
         load_w1(1, 1, "slot_t1", 1)
 
         d_rows = [keep.tile([P, S], F32, name="d_rows%d" % t) for t in range(PACK)]
-        for half in range(2):
+        for half in range(S // BANK):
             cols = slice(half * BANK, (half + 1) * BANK)
             gather_words(1, half)
             d_pass(1, half)
@@ -160,176 +174,168 @@ def tile_list_tariff_spike_scores_kernel(
         mat_t = stage.tile([P, PACK, M], F32, name="mat_t", tag="slot_a", align_bytes=64)
         nc.sync.dma_start(mat_t[:], mat.rearrange("(p t) m -> p t m", t=PACK))
 
-        w1_q = {}
-        w1_s = {}
+        w1_codes = {}
+        w1_scale = {}
         w1_bf = {}
 
-        def round_w1(b, a, on_scalar, pieces):
+        def round_w1(b, a, copy, pieces):
             grouped = ring.tile([P, PACK * PASS], BF16, name="w1_bf", tag="w1_bf", bufs=2, align_bytes=64)
             dst = grouped[:].rearrange("p (t m j) -> p m j t", t=PACK, j=PACK)
             src = w1_raw[(b, a)][:].rearrange("p j (m t) -> p m j t", t=PACK)
             for piece in range(pieces):
-                ms = slice(piece * P // pieces, (piece + 1) * P // pieces)
-                for pair in range(2):
-                    ts = slice(2 * pair, 2 * pair + 2)
-                    if on_scalar:
-                        nc.scalar.copy(dst[:, ms, :, ts], src[:, ms, :, ts])
-                    else:
-                        nc.vector.tensor_copy(dst[:, ms, :, ts], src[:, ms, :, ts])
+                places = slice(piece * P // pieces, (piece + 1) * P // pieces)
+                for pair in range(PACK // 2):
+                    slices = slice(2 * pair, 2 * pair + 2)
+                    copy(dst[:, places, :, slices], src[:, places, :, slices])
             w1_bf[(b, a)] = grouped
 
         def quantise_w1(b, a):
-            codes = keep.tile([P, PASS], U32, name="w1_q%d%d" % (b, a), align_bytes=64)
-            scales = keep.tile([P, PASS], U8, name="w1_s%d%d" % (b, a), align_bytes=64)
-            for pair in range(2):
-                cols = slice(pair * PASS // 2, (pair + 1) * PASS // 2)
+            codes = keep.tile([P, PASS], U32, name="w1_codes%d%d" % (b, a), align_bytes=64)
+            scale = keep.tile([P, PASS], U8, name="w1_scale%d%d" % (b, a), align_bytes=64)
+            for pair in range(PACK // 2):
+                cols = slice(pair * 2 * P, (pair + 1) * 2 * P)
                 nc.vector.quantize_mx(
-                    codes[:, cols].bitcast(FP8X4), scales[:, cols],
+                    codes[:, cols].bitcast(FP8X4), scale[:, cols],
                     w1_bf[(b, a)][:, PACK * cols.start : PACK * cols.stop],
                 )
-            w1_q[(b, a)] = codes
-            w1_s[(b, a)] = scales
+            w1_codes[(b, a)] = codes
+            w1_scale[(b, a)] = scale
 
-        round_w1(0, 0, False, 1)
+        round_w1(0, 0, nc.vector.tensor_copy, 1)
         quantise_w1(0, 0)
-        round_w1(0, 1, False, 2)
+        round_w1(0, 1, nc.vector.tensor_copy, 2)
         quantise_w1(0, 1)
-        round_w1(1, 0, False, 1)
+        round_w1(1, 0, nc.vector.tensor_copy, 1)
         quantise_w1(1, 0)
 
-        h_q = [keep.tile([P, S], U32, name="h_q%d" % b, align_bytes=64) for b in range(2)]
-        h_s = [keep.tile([P, S], U8, name="h_s%d" % b, align_bytes=64) for b in range(2)]
+        h_codes = [keep.tile([P, S], U32, name="h_codes%d" % b, align_bytes=64) for b in range(PASSES)]
+        h_scale = [keep.tile([P, S], U8, name="h_scale%d" % b, align_bytes=64) for b in range(PASSES)]
         e_rows = [keep.tile([P, S], F32, name="e_rows%d" % t) for t in range(PACK)]
-        units = [(b, u) for b in range(2) for u in range(S // UNIT)]
+        steps = [(b, u) for b in range(PASSES) for u in range(UNITS)]
+        last_step = len(steps) - 1
         tanh_of = {}
         h_bf = {}
 
-        def tanh_unit(i):
-            b, u = units[i]
-            if i == len(units) - 1:
+        def tanh_step(i):
+            b, u = steps[i]
+            if i == last_step:
                 th = ring.tile([P, UNIT, PACK], F32, name="th_last", tag="th_last", align_bytes=64)
             else:
                 th = ring.tile([P, UNIT, PACK], F32, name="th", tag="th", bufs=4, align_bytes=64)
             for c in range(UNIT // P):
-                bank = banks[(2 * i + c) % 4]
+                bank = banks[(i * UNIT // P + c) % STAGE1_BANKS]
                 cols = slice(u * UNIT + c * P, u * UNIT + (c + 1) * P)
-                for a in range(2):
+                for a in range(PASSES):
                     for t in range(PACK):
                         rows = slice(t * P, (t + 1) * P)
                         nc.tensor.matmul_mx(
                             bank[:, rows],
-                            lhsT=w1_q[(b, a)][:, rows].bitcast(FP8X4), lhsT_scale=w1_s[(b, a)][:, rows],
-                            rhs=v_words[a][:, cols].bitcast(FP8X4), rhs_scale=v_scales[4 * a :, cols],
-                            start=(a == 0 and t == 0), stop=(a == 1 and t == PACK - 1),
+                            lhsT=w1_codes[(b, a)][:, rows].bitcast(FP8X4), lhsT_scale=w1_scale[(b, a)][:, rows],
+                            rhs=v_codes[a][:, cols].bitcast(FP8X4), rhs_scale=v_scale[4 * a :, cols],
+                            start=(a == 0 and t == 0), stop=(a == PASSES - 1 and t == PACK - 1),
                         )
                 nc.scalar.activation(
                     th[:, c * P : (c + 1) * P, :], bank[:].rearrange("p (t n) -> p n t", t=PACK), ACT.Tanh
                 )
             tanh_of[i] = th
 
-        def gain_unit(i):
-            b, u = units[i]
+        def gain_step(i):
+            b, u = steps[i]
             hb = ring.tile([P, UNIT, PACK], BF16, name="hb", tag="hb", bufs=3, align_bytes=64)
             nc.vector.tensor_tensor(
                 hb[:], tanh_of[i][:], hgain_t[:, b : b + 1, :].to_broadcast([P, UNIT, PACK]), ALU.mult
             )
             h_bf[i] = hb
 
-        def quantise_unit(i):
-            b, u = units[i]
+        def quantise_step(i):
+            b, u = steps[i]
             cols = slice(u * UNIT, (u + 1) * UNIT)
             nc.vector.quantize_mx(
-                h_q[b][:, cols].bitcast(FP8X4), h_s[b][:, cols], h_bf[i][:].rearrange("p n t -> p (n t)")
+                h_codes[b][:, cols].bitcast(FP8X4), h_scale[b][:, cols], h_bf[i][:].rearrange("p n t -> p (n t)")
             )
 
-        def e_pass(out, t, b, cols, start, stop):
+        def e_matmul(out, t, b, cols, start, stop):
             nc.tensor.matmul_mx(
                 out,
-                lhsT=wa_q[:, b, t * P : (t + 1) * P].bitcast(U8).bitcast(FP4X4),
-                lhsT_scale=wa_s[:, b, t * P : (t + 1) * P],
-                rhs=h_q[b][:, cols].bitcast(FP8X4), rhs_scale=h_s[b][:, cols],
+                lhsT=wa_codes[:, b, t * P : (t + 1) * P].bitcast(U8).bitcast(FP4X4),
+                lhsT_scale=wa_scale[:, b, t * P : (t + 1) * P],
+                rhs=h_codes[b][:, cols].bitcast(FP8X4), rhs_scale=h_scale[b][:, cols],
                 start=start, stop=stop,
             )
 
-        def e_place(u, t):
-            if u < 2:
-                return banks[4 + 2 * u + t // 2][:, (t % 2) * UNIT : (t % 2 + 1) * UNIT]
-            return banks[t][:, (u - 2) * UNIT : (u - 1) * UNIT]
+        def early_place(u, t):
+            return banks[STAGE1_BANKS + 2 * u + t // 2][:, (t % 2) * UNIT : (t % 2 + 1) * UNIT]
 
-        def e_first(u):
+        def early_pass(u, b):
             for t in range(PACK):
-                if u < 2:
-                    e_pass(e_place(u, t), t, 0, slice(u * UNIT, (u + 1) * UNIT), t % 2 == 0, False)
-                else:
-                    e_pass(banks[t][:], t, 0, slice(BANK, S), True, False)
+                e_matmul(
+                    early_place(u, t), t, b, slice(u * UNIT, (u + 1) * UNIT),
+                    b == 0 and t % 2 == 0, b == PASSES - 1 and t % 2 == 1,
+                )
 
-        def e_second(u):
+        def early_out(u):
             for t in range(PACK):
-                stop = t % 2 == 1 if u < 2 else u == 3
-                e_pass(e_place(u, t), t, 1, slice(u * UNIT, (u + 1) * UNIT), False, stop)
+                nc.scalar.copy(e_rows[t][:, u * UNIT : (u + 1) * UNIT], early_place(u, t))
 
-        def e_out(u):
-            for t in range(PACK):
-                if u < 2:
-                    nc.scalar.copy(e_rows[t][:, u * UNIT : (u + 1) * UNIT], e_place(u, t))
-                elif t < PACK - 1:
-                    nc.scalar.copy(e_rows[t][:, BANK:], banks[t][:])
-                else:
-                    nc.vector.tensor_copy(e_rows[t][:, BANK:], banks[t][:])
+        mat_gain = keep.tile([P, PACK, M], F32, name="mat_gain")
 
-        matg = keep.tile([P, PACK, M], F32, name="matg")
-        per_block = S // UNIT
-
-        for i in range(len(units)):
-            if i == per_block:
-                round_w1(1, 1, True, 1)
+        for i in range(len(steps)):
+            if i == UNITS:
+                round_w1(1, 1, nc.scalar.copy, 1)
                 quantise_w1(1, 1)
-            tanh_unit(i)
-            gain_unit(i)
+            tanh_step(i)
+            gain_step(i)
             if i > 0:
-                quantise_unit(i - 1)
-            if i == per_block:
-                e_first(0)
-                e_first(1)
+                quantise_step(i - 1)
+            if i == UNITS:
+                early_pass(0, 0)
+                early_pass(1, 0)
                 for t in range(PACK):
-                    nc.vector.tensor_scalar_mul(matg[:, t, :], mat_t[:, t, :], ygain_t[:, t : t + 1])
-        quantise_unit(len(units) - 1)
-        e_second(0)
-        e_out(0)
-        e_second(1)
-        e_out(1)
-        e_first(2)
-        e_second(2)
-        e_second(3)
-        e_out(2)
+                    nc.vector.tensor_scalar_mul(mat_gain[:, t, :], mat_t[:, t, :], ygain_t[:, t : t + 1])
+        quantise_step(last_step)
 
-        y_q = keep.tile([P, M], U32, name="y_q", align_bytes=64)
-        y_s = keep.tile([P, M], U8, name="y_s", align_bytes=64)
+        for u in range(UNITS // 2):
+            early_pass(u, 1)
+            early_out(u)
+        for t in range(PACK):
+            e_matmul(banks[t][:], t, 0, slice(BANK, S), True, False)
+        for u in range(UNITS // 2, UNITS):
+            cols = slice(u * UNIT, (u + 1) * UNIT)
+            for t in range(PACK):
+                e_matmul(banks[t][:, cols.start - BANK : cols.stop - BANK], t, 1, cols, False, u == UNITS - 1)
+        for t in range(PACK - 1):
+            nc.scalar.copy(e_rows[t][:, BANK:], banks[t][:])
+        nc.vector.tensor_copy(e_rows[PACK - 1][:, BANK:], banks[PACK - 1][:])
+
+        y_codes = keep.tile([P, M], U32, name="y_codes", align_bytes=64)
+        y_scale = keep.tile([P, M], U8, name="y_scale", align_bytes=64)
         out_rows = out_0.rearrange("(p t) m -> p t m", t=PACK)
         out_words = out_1[0].rearrange("p m i -> p (m i)").bitcast(I32)
         y = []
+        picked = ring.tile([P, M // HALF, PACK, HALF], F32, name="picked", tag="th_last", align_bytes=64)
         for half in range(M // HALF):
             cols = slice(half * HALF, (half + 1) * HALF)
-            entries = slice(half * HALF // 16, (half + 1) * HALF // 16)
-            picked = ring.tile([P, PACK, HALF], F32, name="picked", tag=["th_last", "look0"][half], align_bytes=64)
             for t in range(PACK):
                 nc.vector.tensor_tensor(
-                    picked[:, t, :], d_rows[t][:].indirect(pos2_t[:, entries]), matg[:, t, cols], ALU.mult
+                    picked[:, half, t, :], d_rows[t][:].indirect(pos2_t[:, entries_of(cols)]),
+                    mat_gain[:, t, cols], ALU.mult,
                 )
             look = ring.tile([P, PACK, HALF], F32, name="look", tag="look%d" % half, align_bytes=64)
             y_half = keep.tile([P, PACK, HALF], F32, name="y%d" % half)
             for t in range(PACK):
                 nc.scalar.activation(
-                    look[:, t, :], e_rows[t][:].indirect(pos1_t[:, entries]), ACT.Exp,
+                    look[:, t, :], e_rows[t][:].indirect(pos1_t[:, entries_of(cols)]), ACT.Exp,
                     bias=shift_t[:, t : t + 1], scale=temp_t[:, t : t + 1],
                 )
                 nc.vector.scalar_tensor_tensor(
-                    y_half[:, t, :], look[:, t, :], neg_ygain[:, t : t + 1], picked[:, t, :], ALU.mult, ALU.add
+                    y_half[:, t, :], look[:, t, :], neg_ygain[:, t : t + 1], picked[:, half, t, :],
+                    ALU.mult, ALU.add,
                 )
                 if t % 2 == 1:
                     nc.sync.dma_start(out_rows[:, t - 1 : t + 1, cols], y_half[:, t - 1 : t + 1, :])
             y.append(y_half)
 
+        runs = HALF // 4
         for half in range(M // HALF):
             cols = slice(half * HALF, (half + 1) * HALF)
             y_bf = keep.tile([P, HALF, PACK], BF16, name="y_bf%d" % half, align_bytes=64)
@@ -338,12 +344,14 @@ def tile_list_tariff_spike_scores_kernel(
             if half == 0:
                 nc.vector.tensor_copy(dst, src)
             else:
-                nc.vector.tensor_copy(dst[:, : HALF // 8], src[:, : HALF // 8])
-                nc.scalar.copy(dst[:, HALF // 8 :], src[:, HALF // 8 :])
-            nc.vector.quantize_mx(y_q[:, cols].bitcast(FP8X4), y_s[:, cols], y_bf[:].rearrange("p m t -> p (m t)"))
-            nc.sync.dma_start(out_words[:, cols], y_q[:, cols].bitcast(I32))
-        for q in range(4):
-            queue = nc.scalar if q % 2 == 0 else nc.sync
+                nc.vector.tensor_copy(dst[:, : runs // 2], src[:, : runs // 2])
+                nc.scalar.copy(dst[:, runs // 2 :], src[:, runs // 2 :])
+            nc.vector.quantize_mx(
+                y_codes[:, cols].bitcast(FP8X4), y_scale[:, cols], y_bf[:].rearrange("p m t -> p (m t)")
+            )
+            nc.sync.dma_start(out_words[:, cols], y_codes[:, cols].bitcast(I32))
+        for q in range(QUADRANTS):
+            queue = nc.scalar if q < QUADRANTS - 1 else nc.sync
             queue.dma_start(
-                out_2[0, 4 * q : 4 * q + 4, :].bitcast(I32), y_s[32 * q : 32 * q + 4, :].bitcast(I32)
+                out_2[0, 4 * q : 4 * q + 4, :].bitcast(I32), y_scale[32 * q : 32 * q + 4, :].bitcast(I32)
             )

from contextlib import ExitStack

import concourse.mybir as mybir

K, H, N, T, S, M = 1024, 1024, 512, 4096, 1024, 512
FLOPS = 2 * K * H * S + 2 * H * N * S + 2 * K * N * S

F32 = mybir.dt.float32
BF16 = mybir.dt.bfloat16
I32 = mybir.dt.int32
U32 = mybir.dt.uint32
U16 = mybir.dt.uint16
U8 = mybir.dt.uint8
FP8X4 = mybir.dt.float8_e4m3fn_x4
FP4X4 = mybir.dt.float4_e2m1fn_x4
ACT = mybir.ActivationFunctionType
ALU = mybir.AluOpType

P = 128
PACK = 4
PASS = P * PACK
PASSES = 2
QUADRANTS = 4
PER_COLUMN = 16
BANK = 512
STAGE1_BANKS = 4
UNIT = 256
UNITS = S // UNIT
HALF = M // 2


def tile_list_tariff_spike_scores_kernel(
    tc, tab_words, tab_scales, offs, w1, hgain, wa_words, wa_scales, wb_words, wb_scales,
    pos1, pos2, temp, shift, mat, ygain, out_0, out_1, out_2,
):
    nc = tc.nc
    with ExitStack() as ctx:
        lists = ctx.enter_context(tc.tile_pool(name="lists", bufs=1))
        keep = ctx.enter_context(tc.tile_pool(name="keep", bufs=1))
        stage = ctx.enter_context(tc.tile_pool(name="stage", bufs=1))
        ring = ctx.enter_context(tc.tile_pool(name="ring", bufs=1))
        psum = ctx.enter_context(tc.psum_pool(name="psum", bufs=1))

        banks = [psum.tile([P, BANK], F32, name="bank%d" % i) for i in range(8)]

        def entries_of(cols):
            return slice(cols.start // PER_COLUMN, cols.stop // PER_COLUMN)

        offs_t = lists.tile([P, S // PER_COLUMN], U16, name="offs_t")
        pos1_t = lists.tile([P, M // PER_COLUMN], U16, name="pos1_t")
        pos2_t = lists.tile([P, M // PER_COLUMN], U16, name="pos2_t")

        tab_scale_rows = stage.tile([P, T], U8, name="tab_scale_rows", tag="slot_c", align_bytes=64)
        wb_scale_rows = stage.tile([P, N], U8, name="wb_scale_rows", tag="slot_b", align_bytes=64)
        wa_scale_rows = keep.tile([P, PASSES, N], U8, name="wa_scale_rows", align_bytes=64)
        nc.gpsimd.memset(tab_scale_rows[:, : T // 2].bitcast(I32), 0)
        nc.vector.memset(tab_scale_rows[:, T // 2 :].bitcast(I32), 0)
        nc.gpsimd.memset(wb_scale_rows[:].bitcast(I32), 0)
        nc.gpsimd.memset(wa_scale_rows[:].bitcast(I32), 0)

        nc.sync.dma_start(offs_t[:], offs)
        nc.sync.dma_start(pos1_t[:], pos1)
        nc.sync.dma_start(pos2_t[:], pos2)
        wb_raw = keep.tile([P, PASSES, N], I32, name="wb_raw", align_bytes=64)
        nc.sync.dma_start(wb_raw[:], wb_words.rearrange("a p c i -> p a (c i)").bitcast(I32))
        wa_raw = keep.tile([P, PASSES, N], U16, name="wa_raw", align_bytes=64)
        nc.sync.dma_start(wa_raw[:].bitcast(I32), wa_words.rearrange("a p c -> p a c").bitcast(I32))

        tab = [stage.tile([P, T], I32, name="tab%d" % a, tag="slot_t%d" % a, align_bytes=64) for a in range(PASSES)]
        tab_src = [tab_words[a].rearrange("p t i -> p (t i)").bitcast(I32) for a in range(PASSES)]
        nc.sync.dma_start(tab[0][:, : T // 2], tab_src[0][:, : T // 2])
        for q in range(QUADRANTS):
            nc.sync.dma_start(
                tab_scale_rows[32 * q : 32 * q + 8, :].bitcast(I32),
                tab_scales[:, 4 * q : 4 * q + 4, :].bitcast(I32),
            )
        nc.sync.dma_start(tab[0][:, T // 2 :], tab_src[0][:, T // 2 :])
        for q in range(QUADRANTS):
            nc.sync.dma_start(
                wb_scale_rows[32 * q : 32 * q + 8, :].bitcast(I32),
                wb_scales[:, 4 * q : 4 * q + 4, :].bitcast(I32),
            )
        nc.sync.dma_start(tab[1][:, : T // 2], tab_src[1][:, : T // 2])
        for q in range(QUADRANTS):
            nc.sync.dma_start(
                wa_scale_rows[32 * q : 32 * q + 4, :, :].bitcast(I32),
                wa_scales[:, 4 * q : 4 * q + 4, :].rearrange("a r n -> r a n").bitcast(I32),
            )
        nc.sync.dma_start(tab[1][:, T // 2 :], tab_src[1][:, T // 2 :])
        ygain_t = keep.tile([P, PACK], F32, name="ygain_t")
        nc.sync.dma_start(ygain_t[:], ygain.rearrange("(p t) -> p t", t=PACK))
        hgain_t = keep.tile([P, PASSES, PACK], F32, name="hgain_t")
        nc.sync.dma_start(hgain_t[:], hgain.rearrange("(b p t) -> p b t", b=PASSES, t=PACK))
        temp_t = keep.tile([P, PACK], F32, name="temp_t")
        nc.sync.dma_start(temp_t[:], temp.rearrange("(p t) -> p t", t=PACK))
        shift_t = keep.tile([P, PACK], F32, name="shift_t")
        nc.sync.dma_start(shift_t[:], shift.rearrange("(p t) -> p t", t=PACK))

        wa_codes = keep.tile([P, PASSES, N], U16, name="wa_codes", align_bytes=64)
        nc.scalar.copy(
            wa_codes[:].rearrange("p a (t g i) -> p a g t i", t=PACK, i=8),
            wa_raw[:].rearrange("p a (g i t) -> p a g t i", t=PACK, i=8),
        )

        neg_ygain = keep.tile([P, PACK], F32, name="neg_ygain")
        nc.scalar.mul(neg_ygain[:], ygain_t[:], -1.0)

        wb_codes = keep.tile([P, PASSES, N], I32, name="wb_codes", align_bytes=64)
        nc.vector.tensor_copy(
            wb_codes[:].rearrange("p a (t m) -> p a m t", t=PACK),
            wb_raw[:].rearrange("p a (m t) -> p a m t", t=PACK),
        )
        v_scale = keep.tile([P, S], U8, name="v_scale", align_bytes=64)
        nc.vector.tensor_copy(v_scale[:], tab_scale_rows[:].indirect(offs_t[:]))

        v_codes = [keep.tile([P, S], U32, name="v_codes%d" % a, align_bytes=64) for a in range(PASSES)]

        def gather_words(a, half):
            cols = slice(half * BANK, (half + 1) * BANK)
            nc.vector.tensor_copy(
                v_codes[a][:, cols], tab[a][:].bitcast(U32).indirect(offs_t[:, entries_of(cols)])
            )

        wb_scale = keep.tile([P, N], U8, name="wb_scale", align_bytes=64)
        nc.vector.tensor_copy(
            wb_scale[:].rearrange("p (t m) -> p m t", t=PACK),
            wb_scale_rows[:].rearrange("p (m t) -> p m t", t=PACK),
        )
        gather_words(0, 0)
        gather_words(0, 1)

        def d_pass(a, half):
            cols = slice(half * BANK, (half + 1) * BANK)
            for t in range(PACK):
                rows = slice(t * P, (t + 1) * P)
                nc.tensor.matmul_mx(
                    banks[PACK * half + t][:],
                    lhsT=wb_codes[:, a, rows].bitcast(FP8X4), lhsT_scale=wb_scale[4 * a :, rows],
                    rhs=v_codes[a][:, cols].bitcast(FP8X4), rhs_scale=v_scale[4 * a :, cols],
                    start=(a == 0), stop=(a == PASSES - 1),
                )

        d_pass(0, 0)
        d_pass(0, 1)
        wa_scale = stage.tile([P, PASSES, N], U8, name="wa_scale", tag="slot_t0", align_bytes=64)
        nc.vector.tensor_copy(
            wa_scale[:].rearrange("p a (t m) -> p a m t", t=PACK),
            wa_scale_rows[:].rearrange("p a (m t) -> p a m t", t=PACK),
        )

        w1_raw = {}

        def load_w1(b, a, tag, pieces):
            raw = stage.tile([P, PACK, PASS], F32, name="w1_raw%d%d" % (b, a), tag=tag, align_bytes=64)
            src = w1[a * PASS : (a + 1) * PASS, b * PASS : (b + 1) * PASS].rearrange("(p j) c -> p j c", j=PACK)
            for piece in range(pieces):
                cols = slice(piece * PASS // pieces, (piece + 1) * PASS // pieces)
                nc.sync.dma_start(raw[:, :, cols], src[:, :, cols])
            w1_raw[(b, a)] = raw

        load_w1(0, 0, "slot_a", 1)
        load_w1(0, 1, "slot_c", 2)
        load_w1(1, 0, "slot_b", 1)
        load_w1(1, 1, "slot_t1", 1)

        d_rows = [keep.tile([P, S], F32, name="d_rows%d" % t) for t in range(PACK)]
        for half in range(S // BANK):
            cols = slice(half * BANK, (half + 1) * BANK)
            gather_words(1, half)
            d_pass(1, half)
            for t in range(PACK):
                nc.scalar.copy(d_rows[t][:, cols], banks[PACK * half + t][:])

        mat_t = stage.tile([P, PACK, M], F32, name="mat_t", tag="slot_a", align_bytes=64)
        nc.sync.dma_start(mat_t[:], mat.rearrange("(p t) m -> p t m", t=PACK))

        w1_codes = {}
        w1_scale = {}
        w1_bf = {}

        def round_w1(b, a, copy, pieces):
            grouped = ring.tile([P, PACK * PASS], BF16, name="w1_bf", tag="w1_bf", bufs=2, align_bytes=64)
            dst = grouped[:].rearrange("p (t m j) -> p m j t", t=PACK, j=PACK)
            src = w1_raw[(b, a)][:].rearrange("p j (m t) -> p m j t", t=PACK)
            for piece in range(pieces):
                places = slice(piece * P // pieces, (piece + 1) * P // pieces)
                for pair in range(PACK // 2):
                    slices = slice(2 * pair, 2 * pair + 2)
                    copy(dst[:, places, :, slices], src[:, places, :, slices])
            w1_bf[(b, a)] = grouped

        def quantise_w1(b, a):
            codes = keep.tile([P, PASS], U32, name="w1_codes%d%d" % (b, a), align_bytes=64)
            scale = keep.tile([P, PASS], U8, name="w1_scale%d%d" % (b, a), align_bytes=64)
            for pair in range(PACK // 2):
                cols = slice(pair * 2 * P, (pair + 1) * 2 * P)
                nc.vector.quantize_mx(
                    codes[:, cols].bitcast(FP8X4), scale[:, cols],
                    w1_bf[(b, a)][:, PACK * cols.start : PACK * cols.stop],
                )
            w1_codes[(b, a)] = codes
            w1_scale[(b, a)] = scale

        round_w1(0, 0, nc.vector.tensor_copy, 1)
        quantise_w1(0, 0)
        round_w1(0, 1, nc.vector.tensor_copy, 2)
        quantise_w1(0, 1)
        round_w1(1, 0, nc.vector.tensor_copy, 1)
        quantise_w1(1, 0)

        h_codes = [keep.tile([P, S], U32, name="h_codes%d" % b, align_bytes=64) for b in range(PASSES)]
        h_scale = [keep.tile([P, S], U8, name="h_scale%d" % b, align_bytes=64) for b in range(PASSES)]
        e_rows = [keep.tile([P, S], F32, name="e_rows%d" % t) for t in range(PACK)]
        steps = [(b, u) for b in range(PASSES) for u in range(UNITS)]
        last_step = len(steps) - 1
        tanh_of = {}
        h_bf = {}

        def tanh_step(i):
            b, u = steps[i]
            if i == last_step:
                th = ring.tile([P, UNIT, PACK], F32, name="th_last", tag="th_last", align_bytes=64)
            else:
                th = ring.tile([P, UNIT, PACK], F32, name="th", tag="th", bufs=4, align_bytes=64)
            for c in range(UNIT // P):
                bank = banks[(i * UNIT // P + c) % STAGE1_BANKS]
                cols = slice(u * UNIT + c * P, u * UNIT + (c + 1) * P)
                for a in range(PASSES):
                    for t in range(PACK):
                        rows = slice(t * P, (t + 1) * P)
                        nc.tensor.matmul_mx(
                            bank[:, rows],
                            lhsT=w1_codes[(b, a)][:, rows].bitcast(FP8X4), lhsT_scale=w1_scale[(b, a)][:, rows],
                            rhs=v_codes[a][:, cols].bitcast(FP8X4), rhs_scale=v_scale[4 * a :, cols],
                            start=(a == 0 and t == 0), stop=(a == PASSES - 1 and t == PACK - 1),
                        )
                nc.scalar.activation(
                    th[:, c * P : (c + 1) * P, :], bank[:].rearrange("p (t n) -> p n t", t=PACK), ACT.Tanh
                )
            tanh_of[i] = th

        def gain_step(i):
            b, u = steps[i]
            hb = ring.tile([P, UNIT, PACK], BF16, name="hb", tag="hb", bufs=3, align_bytes=64)
            nc.vector.tensor_tensor(
                hb[:], tanh_of[i][:], hgain_t[:, b : b + 1, :].to_broadcast([P, UNIT, PACK]), ALU.mult
            )
            h_bf[i] = hb

        def quantise_step(i):
            b, u = steps[i]
            cols = slice(u * UNIT, (u + 1) * UNIT)
            nc.vector.quantize_mx(
                h_codes[b][:, cols].bitcast(FP8X4), h_scale[b][:, cols], h_bf[i][:].rearrange("p n t -> p (n t)")
            )

        def e_matmul(out, t, b, cols, start, stop):
            nc.tensor.matmul_mx(
                out,
                lhsT=wa_codes[:, b, t * P : (t + 1) * P].bitcast(U8).bitcast(FP4X4),
                lhsT_scale=wa_scale[:, b, t * P : (t + 1) * P],
                rhs=h_codes[b][:, cols].bitcast(FP8X4), rhs_scale=h_scale[b][:, cols],
                start=start, stop=stop,
            )

        def early_place(u, t):
            return banks[STAGE1_BANKS + 2 * u + t // 2][:, (t % 2) * UNIT : (t % 2 + 1) * UNIT]

        def early_pass(u, b):
            for t in range(PACK):
                e_matmul(
                    early_place(u, t), t, b, slice(u * UNIT, (u + 1) * UNIT),
                    b == 0 and t % 2 == 0, b == PASSES - 1 and t % 2 == 1,
                )

        def early_out(u):
            for t in range(PACK):
                nc.scalar.copy(e_rows[t][:, u * UNIT : (u + 1) * UNIT], early_place(u, t))

        mat_gain = keep.tile([P, PACK, M], F32, name="mat_gain")

        for i in range(len(steps)):
            if i == UNITS:
                round_w1(1, 1, nc.scalar.copy, 1)
                quantise_w1(1, 1)
            tanh_step(i)
            gain_step(i)
            if i > 0:
                quantise_step(i - 1)
            if i == UNITS:
                early_pass(0, 0)
                early_pass(1, 0)
                for t in range(PACK):
                    nc.vector.tensor_scalar_mul(mat_gain[:, t, :], mat_t[:, t, :], ygain_t[:, t : t + 1])
        quantise_step(last_step)

        for u in range(UNITS // 2):
            early_pass(u, 1)
            early_out(u)
        for t in range(PACK):
            e_matmul(banks[t][:], t, 0, slice(BANK, S), True, False)
        for u in range(UNITS // 2, UNITS):
            cols = slice(u * UNIT, (u + 1) * UNIT)
            for t in range(PACK):
                e_matmul(banks[t][:, cols.start - BANK : cols.stop - BANK], t, 1, cols, False, u == UNITS - 1)
        for t in range(PACK - 1):
            nc.scalar.copy(e_rows[t][:, BANK:], banks[t][:])
        nc.vector.tensor_copy(e_rows[PACK - 1][:, BANK:], banks[PACK - 1][:])

        y_codes = keep.tile([P, M], U32, name="y_codes", align_bytes=64)
        y_scale = keep.tile([P, M], U8, name="y_scale", align_bytes=64)
        out_rows = out_0.rearrange("(p t) m -> p t m", t=PACK)
        out_words = out_1[0].rearrange("p m i -> p (m i)").bitcast(I32)
        y = []
        picked = ring.tile([P, M // HALF, PACK, HALF], F32, name="picked", tag="th_last", align_bytes=64)
        for half in range(M // HALF):
            cols = slice(half * HALF, (half + 1) * HALF)
            for t in range(PACK):
                nc.vector.tensor_tensor(
                    picked[:, half, t, :], d_rows[t][:].indirect(pos2_t[:, entries_of(cols)]),
                    mat_gain[:, t, cols], ALU.mult,
                )
            look = ring.tile([P, PACK, HALF], F32, name="look", tag="look%d" % half, align_bytes=64)
            y_half = keep.tile([P, PACK, HALF], F32, name="y%d" % half)
            for t in range(PACK):
                nc.scalar.activation(
                    look[:, t, :], e_rows[t][:].indirect(pos1_t[:, entries_of(cols)]), ACT.Exp,
                    bias=shift_t[:, t : t + 1], scale=temp_t[:, t : t + 1],
                )
                nc.vector.scalar_tensor_tensor(
                    y_half[:, t, :], look[:, t, :], neg_ygain[:, t : t + 1], picked[:, half, t, :],
                    ALU.mult, ALU.add,
                )
                if t % 2 == 1:
                    nc.sync.dma_start(out_rows[:, t - 1 : t + 1, cols], y_half[:, t - 1 : t + 1, :])
            y.append(y_half)

        runs = HALF // 4
        for half in range(M // HALF):
            cols = slice(half * HALF, (half + 1) * HALF)
            y_bf = keep.tile([P, HALF, PACK], BF16, name="y_bf%d" % half, align_bytes=64)
            src = y[half][:].rearrange("p t (c i) -> p c t i", i=4)
            dst = y_bf[:].rearrange("p (c i) t -> p c t i", i=4)
            if half == 0:
                nc.vector.tensor_copy(dst, src)
            else:
                nc.vector.tensor_copy(dst[:, : runs // 2], src[:, : runs // 2])
                nc.scalar.copy(dst[:, runs // 2 :], src[:, runs // 2 :])
            nc.vector.quantize_mx(
                y_codes[:, cols].bitcast(FP8X4), y_scale[:, cols], y_bf[:].rearrange("p m t -> p (m t)")
            )
            nc.sync.dma_start(out_words[:, cols], y_codes[:, cols].bitcast(I32))
        for q in range(QUADRANTS):
            queue = nc.scalar if q < QUADRANTS - 1 else nc.sync
            queue.dma_start(
                out_2[0, 4 * q : 4 * q + 4, :].bitcast(I32), y_scale[32 * q : 32 * q + 4, :].bitcast(I32)
            )
